import numpy as np, ml_dtypes
CORES = [23,119,17,113]
N = 4
BF = ml_dtypes.bfloat16
def gentries(a):
    return np.ascontiguousarray(a.reshape(8, 16, -1).transpose(0, 2, 1)).reshape(8, -1)
def gtable(e):
    e = np.asarray(e); return np.ascontiguousarray(e.reshape(8, -1, 16).transpose(0, 2, 1)).reshape(128, -1).astype(np.int32)
V, W, G, CAP, ST, L, M, RO = 3072, 3840, 256, 64, 12, 256, 3, 5
TOP = 61440 + W - 1
def pick(rng, shape):
    a = rng.integers(0, W, shape); b = ST * rng.integers(0, L, shape) + rng.integers(0, M, shape)
    return np.where(rng.random(shape) < 0.5, b, a)
def parts(rng):
    x = (rng.integers(1, 257, (N, 8, 1, W)) * rng.random((N, 8, 16, W))).astype(np.int64)
    w = np.minimum(rng.integers(0, 16, (N, 8, 16, V)), rng.integers(3, 16, (N, 8, 1, V)))
    k = 4096 * w + pick(rng, (N, 8, 16, V))
    f = (rng.random((N, 8, V)) < rng.choice(np.array([0.3, 0.5, 0.7]), (N, 8, 1))).astype(np.int64)
    t = np.where(rng.random((N, 8, M * L)) < 0.6, rng.integers(0, 2601, (N, 8, M * L)), rng.integers(0, 601, (N, 8, M * L)))
    s = np.ascontiguousarray(np.argsort(rng.random((N, 8, N - 1, L)), axis=-1)[..., :G])
    return x, k, f, t, s
def pack(x, k, f, t, s):
    return {"x0": np.ascontiguousarray(x.reshape(N, 128, W)).astype(np.float32).astype(BF), "kt": np.ascontiguousarray(k.reshape(N, 128, V)).astype(np.int32),
            "f0": np.ascontiguousarray(f).astype(np.int32), "th": np.ascontiguousarray(t).astype(np.int32), "shw": np.stack([gtable(a.reshape(8, -1)) for a in s])}
def setup_inputs(rng):
    return pack(*parts(rng))
def setup_inputs_spread(rng):
    x, k, f, t, s = parts(rng)
    x = np.minimum(np.exp2(8.2 * rng.random((N, 8, 1, W)) * rng.random((N, 8, 16, W))).astype(np.int64) - 1, 255)
    w = np.minimum((16 * rng.random((N, 8, 16, V)) ** rng.choice(np.array([0.3, 1.0, 3.0]), (N, 8, 1, V))).astype(np.int64), 15)
    o = np.argsort(rng.random((N, 8, W)), axis=-1); j = np.minimum((W * rng.random((N, 8, 16 * V)) ** 3).astype(np.int64), W - 1)
    k = 4096 * w + np.take_along_axis(o, j, 2).reshape(N, 8, 16, V)
    f = (rng.random((N, 8, V)) < rng.choice(np.array([0.05, 0.5, 0.95]), (N, 8, 1))).astype(np.int64)
    t = np.minimum(np.exp2(12 * rng.random((N, 8, M * L))).astype(np.int64) - 1, 4080)
    s = np.minimum((L * rng.random((N, 8, N - 1, G)) ** 2).astype(np.int64), L - 1)
    return pack(x, k, f, t, s)
def setup_inputs_ends(rng):
    last = ST * (L - 1) + M - 1
    x = 255 * rng.integers(0, 2, (N, 8, 16, W)); kind = rng.integers(0, 3, (N, 8, 1, W))
    x = np.where(kind == 0, 0, np.where(kind == 1, 255, x))
    x[..., W - 1] = 255; x[:, 3, :, W - 1] = 255 * rng.integers(0, 2, (N, 16)); x[:, 5, :, W - 1] = 0
    k = TOP * rng.integers(0, 2, (N, 8, 16, V)); kind = rng.integers(0, 10, (N, 8, 1, V))
    e = 61440 * rng.integers(0, 2, (N, 8, 16, V)) + rng.choice(np.array([0, 1, V - 1, last, V, W - 1]), (N, 8, 16, V))
    k = np.where(kind < 2, 0, np.where(kind < 4, TOP, np.where(kind < 7, k, e)))
    for m in range(M):
        for i in (1, 2, L - 1):
            x[..., ST * i + m] = 0; k[..., ST * i + m] = TOP
        x[..., ST * (L - 2) + m] = 0; k[..., ST * (L - 2) + m] = 0
        x[..., ST * 3 + m] = 255; k[..., ST * 3 + m] = 0
    k[..., V - 1] = TOP
    f = rng.integers(0, 2, (N, 8, V)); f[:, ::2, V - 1] = 1
    t = 4080 * rng.integers(0, 2, (N, 8, M * L))
    z = ST * np.arange(L); xv = x[..., z]; flat = np.all(xv == xv[:, :, :1], axis=2)
    f[..., z] = np.where(flat, 1, f[..., z]); t[..., :L] = 4080 * (1 - f[..., z])
    f[1::2, 7, ST * (L - 1)] = 0; t[1::2, 7, L - 1] = 4080
    for m in range(1, M):
        t[..., m * L + 2] = 4080; t[..., m * L + L - 1] = 4080
    s = np.where(rng.random((N, 8, N - 1, G)) < 0.75, (L - 1) * rng.integers(0, 2, (N, 8, N - 1, G)), rng.integers(0, L, (N, 8, N - 1, G)))
    return pack(x, k, f, t, s)
def setup_inputs_corners(rng):
    x, k, f, t, s = parts(rng); own = np.arange(V); h = L // 2
    k = 4096 * rng.choice(np.array([0, 15, 15]), (N, 8, 16, V)) + (k & 4095)
    f[:, 2] = 0; f[:, 4] = 1; f[:, 6] = 1
    k[:, 1] = (k[:, 1] & 61440) + own; k[:, 3] = k[:, 3] & 61440
    k[:, 5] = (k[:, 5] & 61440) + rng.choice(np.array([V - 1, W - 1]), (N, 16, V)); k[:, 6] = 61440 + np.maximum(own - 1, 0)
    t = np.where(rng.random(t.shape) < 0.3, 4080 * rng.integers(0, 2, t.shape), t)
    x[..., W - 1] = rng.integers(2, 256, (N, 8, 16))
    for q in range(N):
        for g in range(8):
            o = rng.permutation(L); a, b = o[:h], o[h:]; xx = x[q, g]; kk = k[q, g]
            xx[:, ST * a] = 0; kk[rng.integers(0, 16, h), ST * a] = TOP
            kk[:, ST * b] = 61440 + ST * b
            b2 = b[:h // 4]; u = rng.integers(0, 2, (16, h // 4)); u[0] = 1
            xx[:, ST * b2] = xx[:, W - 1:W] - u; kk[:, ST * b2] = TOP; t[q, g, b2] = 0
            for d in range(N - 1):
                n = int(rng.choice(np.array([0, 1, CAP - 1, CAP, CAP + 1, G])))
                if (q == 0 and d == 0) or (q == N - 1 and d == N - 2): n = (CAP, CAP + 1, G, CAP - 1, 1, 0, CAP + 1, CAP)[g]
                s[q, g, d] = rng.permutation(np.concatenate([a[rng.integers(0, h, n)], b[rng.integers(0, h, G - n)]]))
    return pack(x, k, f, t, s)
def setup_inputs_crowd(rng):
    x, k, f, t, s = parts(rng); z = ST * np.arange(L); h2 = L // 2
    for q in range(N):
        for g in range(8):
            xx = x[q, g]; kk = k[q, g]
            if g % 2 == 1:
                hub = int(ST * rng.integers(0, L) + M - 1); was = np.array(kk); j = int(rng.integers(0, V)); one = int(rng.integers(0, L))
                kk[:] = (kk & 61440) + hub; kk[:, hub] = was[:, hub]; s[q, g] = one
                if g < 4: f[q, g, hub] = 1
                if g % 4 == 3:
                    kk[:, j] = was[:, j]; s[q, g, :, G - 1] = (one + 1) % L
            flip = np.ones(L, bool)
            if q % 4 == 1 and g == 7: flip[L - 1] = False
            if q % 4 == 2 and g % 2 == 1: flip[int(rng.integers(0, L))] = False
            if q % 4 == 3:
                flip[:] = g == 0
                flip[int(rng.integers(0, L))] = False
            xx[0, z] = rng.integers(1, 255, L)
            t[q, g, :L] = np.where(flip == (f[q, g, z] == 1), 0, 4080)
            xx[:, V - 1] = 255; f[q, g, V - 1] = 0
            i = rng.permutation(L)[:h2]; u = rng.integers(4, 255, (16, h2))
            xx[:, ST * i + 1] = 255 - u; kk[:, ST * i + 1] = 61440 + V - 1
            t[q, g, L + i] = np.add.reduce(u, axis=0) - rng.integers(0, 64, h2)
    return pack(x, k, f, t, s)
def setup_inputs_ties(rng):
    x, k, f, t, s = parts(rng); h = L // 2
    rec = 4096 * rng.integers(0, 16, (N, 8, 16, 1)) + pick(rng, (N, 8, 16, 1))
    lane = (np.arange(V) % ST) < M
    e = np.where(lane & (rng.random((N, 8, 16, V)) < 0.5), 61440 + pick(rng, (N, 8, 16, V)), rec)
    k[:, 1::2] = e[:, 1::2]; k[:, 2, 8:] = k[:, 2, :8]; k[:, 4, 1:] = np.where(rng.random((N, 15, V)) < 0.5, k[:, 4, :1], k[:, 4, 1:])
    x[..., V - 1] = 255; f[..., V - 1] = 0
    for q in range(N):
        for g in range(8):
            i = rng.permutation(L)[:h]; u = rng.integers(4, 255, (16, h)); xx = x[q, g]; kk = k[q, g]
            xx[:, ST * i] = 255 - u; kk[:, ST * i] = 61440 + V - 1
            t[q, g, i] = np.add.reduce(u, axis=0) + rng.integers(-1, 2, h)
    return pack(x, k, f, t, s)
def check_inputs(d):
    bad = []
    for a, lo, hi in (("x0", 0, 255), ("kt", 0, TOP), ("f0", 0, 1), ("th", 0, 4080), ("shw", 0, L - 1)):
        v = np.asarray(d[a]).astype(np.float64)
        if not (np.min(v) >= lo and np.max(v) <= hi): bad.append("range of " + a)
    v = np.asarray(d["x0"]).astype(np.float64)
    if not np.all(v == np.floor(v)): bad.append("whole numbers of x0")
    if np.max(np.asarray(d["kt"]).astype(np.int64) & 4095) >= W: bad.append("masters of kt")
    return bad
def reference(x0, kt, f0, th, shw):
    x = x0.astype(np.float32).astype(np.int64).reshape(N, 8, 16, W)
    k0 = kt.astype(np.int64).reshape(N, 8, 16, V); k = np.array(k0)
    f = np.zeros((N, 8, W), np.int64); f[..., :V] = f0
    o = np.zeros((N, 8, 16, V), np.int64) + np.arange(V)
    lim = th.astype(np.int64).reshape(N, 8, M, L)
    s = np.stack([gentries(a) for a in shw]).astype(np.int64).reshape(N, 8, N - 1, G)
    num = np.zeros(N, np.int64)
    for rnd in range(RO):
        m = rnd % M; v = ST * np.arange(L) + m
        ov = o[..., v]; fo = np.take_along_axis(f, ov.reshape(N, 8, 16 * L), 2).reshape(N, 8, 16, L)
        back = (ov != v) & (fo == 0)
        kv = np.where(back, k0[..., v], k[..., v]); ov = np.where(back, v, ov); k[..., v] = kv
        c = kv & 4095; w = kv >> 12
        fc = np.take_along_axis(f, c.reshape(N, 8, 16 * L), 2).reshape(N, 8, 16, L)
        best = np.where(fc == 0, kv, -1)
        for j in range(16):
            e = np.take_along_axis(k, np.minimum(c[:, :, j], V - 1)[:, :, None, :], 3)
            cand = 4096 * np.minimum(w[:, :, j][:, :, None, :], e >> 12) + (e & 4095)
            win = (fc[:, :, j] == 1)[:, :, None, :] & (cand > best)
            best = np.where(win, cand, best); ov = np.where(win, c[:, :, j][:, :, None, :], ov)
        k[..., v] = best; o[..., v] = ov
        c = best & 4095; w = best >> 12; y = np.zeros((N, 8, 16, L), np.int64)
        for j in range(16):
            e = np.take_along_axis(x, c[:, :, j][:, :, None, :], 3)
            y = np.maximum(y, np.minimum(e, 17 * w[:, :, j][:, :, None, :]))
        xv = x[..., v]; dist = np.add.reduce(np.abs(xv - y), axis=2)
        st = (dist < lim[:, :, m] + (num & 63)[:, None, None]).astype(np.int64)
        nx = np.where((st == 1)[:, :, None, :], y, (xv + y) >> 1)
        num = np.add.reduce((st != f[..., v]).astype(np.int64).reshape(N, 8 * L), axis=1)
        f[..., v] = st; x[..., v] = nx
        ch = np.any(nx != xv, axis=2).astype(np.int64)
        for a in range(N):
            for d in range(N - 1):
                q = (a + 1 + d) % N; ix = s[q, :, d]; h = np.take_along_axis(ch[q], ix, 1)
                go = (h == 1) & (np.add.accumulate(h, axis=1) - h < CAP); lo = V + d * G
                x[a, :, :, lo:lo + G] = np.where(go[:, None, :], np.take_along_axis(nx[q], ix[:, None, :], 2), x[a, :, :, lo:lo + G])
    yk = np.add.reduce(k.reshape(N, 128, L, ST)[..., :M], axis=3); yo = np.add.reduce(o.reshape(N, 128, L, ST)[..., :M], axis=3)
    return {"yx": x.reshape(N, 128, W).astype(np.float32).astype(BF), "yf": f[..., :V].astype(np.float32), "yk": yk.astype(np.float32), "yo": yo.astype(np.float32)}

@@ -1,0 +1,740 @@
+from concourse.bass import DstId, RemoteDMATransfer
+from concourse.mybir import AluOpType as OP, ActivationFunctionType as AF
+
+N, NV, NW, NL, ST, RO = 4, 3072, 3840, 256, 12, 5
+S = 4096
+F32, BF, I32, U16 = "float32", "bfloat16", "int32", "uint16"
+
+
+def _sb(n, d):
+    return ("sbuf", [128, n], d)
+
+
+SCRATCH = {
+    "ps": ("psum", [128, 4096], F32),
+    "ktb": _sb(NV, I32), "gt": _sb(NW, F32), "xt0": _sb(NW, BF), "xt1": _sb(NW, BF),
+    "fst": _sb(192, I32), "f2": _sb(384, BF), "ffl": _sb(192, F32), "ff": _sb(NV, F32),
+    "thi": _sb(48, I32), "thc": _sb(48, F32), "thf": _sb(768, F32), "shi": _sb(48, I32), "shu": _sb(48, U16),
+    "gg": _sb(4096, F32), "zz": _sb(4096, BF), "rr": _sb(4096, BF), "so": _sb(4096, F32),
+    "xg": _sb(4096, BF), "og": _sb(4096, BF), "ot0": _sb(4352, BF), "ot1": _sb(4352, BF),
+    "pi": _sb(4, I32), "col": _sb(32, F32), "q128": _sb(128, F32), "qg": _sb(128, F32), "m16": _sb(16, F32), "m8": _sb(8, F32),
+    "eye": _sb(128, BF), "blk": _sb(128, BF), "b01": _sb(128, BF), "mats": _sb(6 * 128, BF),
+    "sw2": _sb(1024, BF), "sw3": _sb(1024, BF), "dga": _sb(2048, BF), "dgb": _sb(2048, BF), "slo": _sb(2048, BF),
+    "thm": _sb(128, F32), "cnm": _sb(128, F32), "lc": _sb(128, BF), "cv": _sb(1280, BF),
+    "rs3": _sb(1024, BF), "rs5": _sb(768, BF), "va": _sb(256, BF), "vb": _sb(768, BF), "vt": _sb(512, F32), "bas": _sb(48, F32),
+    "ci": _sb(256, I32), "c16": _sb(512, U16), "own": _sb(512, F32), "w2a": _sb(1024, BF), "w2b": _sb(512, BF),
+    "chi": _sb(256, BF), "clo": _sb(256, BF), "kp": _sb(5 * 256, I32), "kin": _sb(256, I32),
+    "cj": _sb(256, I32), "d16": _sb(256, U16), "fd": _sb(5 * 256, BF), "fo": _sb(256, BF),
+    "mxv": _sb(256, BF), "tt4": _sb(256, BF), "yc": _sb(256, BF), "wn0": _sb(1024, BF), "wn1": _sb(1024, BF),
+    "ne": _sb(256, BF), "chs": _sb(256, BF), "hh": _sb(768, BF), "cum": _sb(768, BF),
+    "q48": _sb(48, F32), "r48": _sb(48, F32), "o48": _sb(48, U16),
+    "ab": _sb(256, BF), "cnt": _sb(4, F32), "qi": _sb(4, I32), "am": _sb(4, F32),
+    "fra": _sb(256, F32), "kb": _sb(512, BF), "oo": _sb(512, U16), "o16": _sb(512, U16), "dov": _sb(512, F32),
+    "dkn": _sb(512, I32), "dkm": _sb(512, F32), "frn": _sb(512, BF),
+    "yob": _sb(256, F32), "ykb": _sb(256, F32), "yka": _sb(256, F32),
+}
+ALIAS = {"fg": "xg", "t3": "zz", "s3": "rr"}
+DMA_GROUPS = ["lf", "lk0", "lk1", "lk2", "lk3", "lt", "ls", "lxg", "lx0", "lx1", "dff", "dva", "dth", "ot_0", "ot_1", "ot_2", "ot_3", "ot_4",
+              "oyx", "oyg", "oyf", "oyk", "oyo"]
+SEMAPHORES = (["eV", "eS", "eP", "eG"] + DMA_GROUPS + ["snd%d" % t for t in range(RO + 1)] + ["arr%d" % t for t in range(RO + 1)])
+
+TUNE = {"look": 200.0, "alpha": 3.0, "gather": 1.56, "fv": 2, "gv": 24, "rs": 0}
+ORDER = [
+17,10,15,16,18,19,0,21,22,11,12,24,20,26,27,59,23,25,38,33,40,39,48,49,34,44,50,35,31,32,37,81,85,29,74,70,149,86,106,1,117,2,3,4,5,8,6,53,36,28,42,115,41,114,45,118,75,73,63,71,80,7,62,65,64,9,144,150,143,148,147,113,109,110,151,160,161,46,119,121,43,116,123,125,122,124,47,120,127,132,79,72,129,130,131,139,126,133,134,135,137,136,138,140,77,111,128,51,54,145,165,166,52,55,236,57,56,171,175,58,176,178,177,14,154,162,163,172,153,179,180,181,182,173,201,202,203,68,174,61,66,67,168,170,247,184,186,185,69,83,60,183,107,103,105,82,188,205,209,167,141,237,155,206,169,187,189,30,190,192,195,213,196,112,84,193,194,204,210,208,207,214,191,215,216,242,221,217,222,13,152,245,199,197,198,230,200,212,211,233,234,219,220,227,228,226,248,235,251,232,258,231,259,229,252,257,157,260,104,261,238,218,108,223,224,263,262,240,241,249,250,264,265,239,225,158,156,243,244,246,255,254,253,256,266,267,268,284,288,142,289,291,269,76,270,271,290,285,292,296,286,273,363,164,319,275,297,298,287,146,320,322,362,305,355,276,277,302,304,303,293,295,278,356,279,78,280,281,361,88,91,323,299,300,294,324,306,364,307,272,308,357,313,311,101,90,89,93,360,98,312,282,283,354,314,321,328,317,318,325,326,332,327,331,309,333,301,310,334,336,339,335,337,99,315,316,348,385,330,386,338,345,92,341,102,95,342,329,350,340,352,343,365,159,367,369,351,366,100,87,94,97,96,344,346,370,353,368,347,349,374,373,379,387,380,381,382,358,274,359,372,371,376,388,391,392,389,375,481,480,383,384,393,394,377,378,390,395,396,397,398,411,415,416,400,412,424,402,418,417,425,426,399,419,403,404,420,421,429,431,430,422,423,405,406,427,407,413,445,414,449,408,409,410,446,447,450,452,483,482,549,433,432,428,434,435,439,436,437,438,440,451,458,448,454,453,457,459,460,461,464,442,456,441,443,473,465,493,444,455,476,462,466,463,469,467,468,474,475,470,478,472,486,477,471,484,488,620,622,487,485,494,495,496,479,497,499,500,504,516,503,515,506,518,505,490,489,501,507,491,492,498,517,519,520,522,621,523,401,508,509,525,527,528,510,511,513,535,524,521,526,550,544,551,547,552,530,531,563,534,529,533,536,532,537,512,554,555,556,557,538,558,559,545,562,539,553,623,686,568,570,569,560,561,540,584,588,592,541,542,543,585,587,586,589,591,590,572,564,514,571,546,573,574,578,579,575,596,576,577,565,580,581,593,597,598,630,582,612,599,603,600,604,595,594,583,615,601,602,609,613,566,617,616,610,608,624,567,625,614,631,611,605,626,627,635,502,606,607,634,632,548,618,619,633,636,637,640,642,628,629,638,761,760,643,655,652,641,644,653,654,656,657,659,662,664,660,665,645,646,647,648,650,672,661,658,663,688,681,684,669,667,700,666,670,668,671,673,674,687,691,692,694,693,695,696,697,698,675,676,705,706,707,690,651,639,689,701,677,678,762,763,679,680,699,721,722,649,724,725,729,723,726,709,727,728,708,710,733,711,715,716,713,714,718,682,717,730,732,734,683,735,712,736,740,741,770,702,703,737,704,719,749,731,771,720,752,738,739,745,746,751,747,764,685,742,743,744,750,768,753,765,748,766,754,767,755,772,773,756,757,774,800,775,799,798,776,779,769,780,781,782,783,785,788,758,759,784,786,787,789,790,791,792,793,794,801,805,777,778,802,803,804,806,807,795,796,797,808,809
+]
+_ORDER = {}
+
+
+def _arrange(ops):
+    key = (len(ops), str(sorted(TUNE.items())))
+    if key in _ORDER:
+        return [ops[n] for n in _ORDER[key]]
+    units, of = [], []
+    for n, o in enumerate(ops):
+        if o.get("join"):
+            units[-1].append(n)
+        else:
+            units.append([n])
+        of.append(len(units) - 1)
+    members = {}
+    for n, o in enumerate(ops):
+        if o["grp"] is not None:
+            members.setdefault(o["grp"], []).append(of[n])
+    pred = [set() for _ in units]
+    hist = {}
+    for n, o in enumerate(ops):
+        u = of[n]
+        for (regs, wr) in ((o["r"], False), (o["w"] + o.get("lock", []), True)):
+            for (name, lo, hi) in regs:
+                for (m, lo2, hi2, wr2) in hist.get(name, []):
+                    if (wr or wr2) and lo < hi2 and lo2 < hi:
+                        p = ops[m]
+                        if p["grp"] is None:
+                            pred[u].add(of[m])
+                        elif p["grp"] != o["grp"]:
+                            pred[u].update(members[p["grp"]])
+        if o["q"] is None:
+            pred[u].update(members["snd" + o["grp"][3:]])
+        if o.get("final"):
+            pred[u].update(range(u))
+        pred[u].discard(u)
+        for (regs, wr) in ((o["r"], False), (o["w"] + o.get("lock", []), True)):
+            for (name, lo, hi) in regs:
+                h = hist.setdefault(name, [])
+                if wr and not o.get("part"):
+                    h[:] = [e for e in h if not (lo <= e[1] and e[2] <= hi)]
+                h.append((n, lo, hi, wr))
+    hold = [sum(ops[n]["hold"] for n in us) for us in units]
+    late = [ops[us[-1]]["late"] for us in units]
+    eng = [ops[us[0]]["q"] for us in units]
+    banks = [set(b for n in us for (name, lo, hi) in ops[n]["r"] + ops[n]["w"] if name == "ps" for b in range(lo // 512, (hi - 1) // 512 + 1))
+             for us in units]
+    succ = [[] for _ in units]
+    for u, ps in enumerate(pred):
+        for p in ps:
+            succ[p].append(u)
+    _ORDER["graph"] = (units, pred, succ, eng, banks, ops)
+    fixed = TUNE.get("fixed", ORDER)
+    if fixed:
+        place = {u: j for j, u in enumerate(fixed)}
+        assert sorted(fixed) == list(range(len(units))) and all(place[p] < place[u] for u, ps in enumerate(pred) for p in ps)
+        _ORDER[key] = [n for u in fixed for n in units[u]]
+        return [ops[n] for n in _ORDER[key]]
+    level = [0.0] * len(units)
+    for u in range(len(units) - 1, -1, -1):
+        level[u] = hold[u] + late[u] + max([level[s] + 60.0 for s in succ[u]], default=0.0)
+    left = [len(p) for p in pred]
+    ready = [u for u in range(len(units)) if not left[u]]
+    done, free, bank, order = {}, {}, {}, []
+    moving = [0.0]
+
+    def start(u):
+        t = max([done[p] + (0.0 if eng[p] == eng[u] == "P" else 60.0) for p in pred[u]], default=0.0)
+        for b in banks[u]:
+            if b in bank and bank[b][0] != eng[u]:
+                t = max(t, bank[b][1] + 60.0)
+        return max(t, free.get(eng[u], 0.0))
+
+    while ready:
+        est = {u: start(u) for u in ready}
+        first = min(ready, key=lambda u: (est[u], -level[u]))
+        u = max((v for v in ready if eng[v] == eng[first] and est[v] <= est[first] + TUNE["look"]),
+                key=lambda v: level[v] - TUNE["alpha"] * (est[v] - est[first]))
+        t = est[u]
+        done[u] = t + hold[u] + late[u]
+        if ops[units[u][0]].get("move"):
+            moving[0] = max(moving[0], t + 1500.0) + ops[units[u][0]]["move"]
+            done[u] = moving[0] + 500.0
+        if eng[u] is not None:
+            free[eng[u]] = t + hold[u]
+        for b in banks[u]:
+            bank[b] = (eng[u], done[u])
+        order += units[u]
+        ready.remove(u)
+        for s in succ[u]:
+            left[s] -= 1
+            if not left[s]:
+                ready.append(s)
+    _ORDER[key] = order
+    return [ops[n] for n in order]
+
+
+def _emit(g, T, ops):
+    queues = {"V": g.vector, "S": g.scalar, "P": g.tensor, "G": g, "Y": g.sync}
+    hist = {}
+    total = {}
+    for o in ops:
+        if o["grp"] is not None:
+            total[o["grp"]] = total.get(o["grp"], 0) + o["inc"]
+    known = {q: ({}, set()) for q in queues}
+    after = {}
+    gclock = {}
+    waited = set()
+    for n, o in enumerate(ops):
+        q = o["q"]
+        deps = set()
+        for (regs, wr) in ((o["r"], False), (o["w"], True)):
+            for (name, lo, hi) in regs:
+                for (m, lo2, hi2, wr2) in hist.get(name, []):
+                    p = ops[m]
+                    same = p["q"] == q and p["grp"] is None and o["grp"] is None
+                    if name == "ps" and not same:
+                        hit = lo // 512 <= (hi2 - 1) // 512 and lo2 // 512 <= (hi - 1) // 512
+                    else:
+                        hit = (wr or wr2) and lo < hi2 and lo2 < hi
+                    if hit and not (same and q == "P") and not (p["grp"] is not None and p["grp"] == o["grp"]):
+                        deps.add(m)
+        if o.get("final"):
+            deps = set(m for m, p in enumerate(ops[:n]) if p["grp"] is not None and p["grp"] not in waited)
+        o["waits"] = []
+        if q is not None:
+            ck, gs = known[q]
+            for m in sorted(deps, reverse=True):
+                p = ops[m]
+                if p["grp"] is not None:
+                    if p["grp"] in gs:
+                        continue
+                    o["waits"].append(("g", p["grp"]))
+                    waited.add(p["grp"])
+                    c2, g2 = gclock[p["grp"]]
+                    gs.add(p["grp"])
+                else:
+                    if ck.get(p["q"], -1) >= m:
+                        continue
+                    o["waits"].append(("e", m))
+                    p["sig"] = True
+                    c2, g2 = after[m]
+                for k, v in c2.items():
+                    ck[k] = max(ck.get(k, -1), v)
+                gs.update(g2)
+            if o["grp"] is None:
+                c = dict(ck)
+                c[q] = n
+                after[n] = (c, set(gs))
+            else:
+                assert o["grp"] not in waited
+                c0, g0 = gclock.get(o["grp"], ({}, set()))
+                c = dict(c0)
+                for k, v in ck.items():
+                    c[k] = max(c.get(k, -1), v)
+                gclock[o["grp"]] = (c, set(g0) | set(gs))
+        else:
+            gclock[o["grp"]] = ({}, set())
+        for (regs, wr) in ((o["r"], False), (o["w"], True)):
+            for (name, lo, hi) in regs:
+                h = hist.setdefault(name, [])
+                if wr and name != "ps" and not o.get("part"):
+                    h[:] = [e for e in h if not (lo <= e[1] and e[2] <= hi)]
+                h.append((n, lo, hi, wr))
+    count = {}
+    for o in ops:
+        if o.get("sig"):
+            count[o["q"]] = count.get(o["q"], 0) + 1
+            o["cnt"] = count[o["q"]]
+    for o in ops:
+        if o["q"] is None:
+            continue
+        e = queues[o["q"]]
+        best = {}
+        for kind, x in o["waits"]:
+            if kind == "g":
+                best[x] = total[x]
+            else:
+                s = "e" + ops[x]["q"]
+                best[s] = max(best.get(s, 0), ops[x]["cnt"])
+        for s, v in best.items():
+            e.wait_ge(T.sem[s], v)
+        if o["fn"] is None:
+            continue
+        ins = o["fn"](e)
+        if o["grp"] is not None:
+            if o["dma"]:
+                ins.then_inc(T.sem[o["grp"]], 16)
+        elif o.get("sig"):
+            ins.then_inc(T.sem["e" + o["q"]], 1)
+
+
+def rank_program(g, core, T, topo):
+    rank = T.rank_of(core)
+    if rank is None:
+        return
+    ops = []
+
+    def a(name, lo=0, hi=None, st=1, p=None):
+        name = ALIAS.get(name, name)
+        t = T[name]
+        hi = t.shape[1] if hi is None else hi
+        ap = t[slice(None) if p is None else p, slice(lo, hi) if st == 1 else slice(lo, hi, st)]
+        return (ap, [(name, lo, hi)], st != 1 or p is not None, len(range(lo, hi, st)), SCRATCH[name][2])
+
+    def ind(win, off):
+        return (win[0].indirect(off[0]), win[1] + off[1], False, 0, win[4])
+
+    def hbm(ap):
+        return (ap, [], False, 2, None)
+
+    def val(x):
+        return x[0] if isinstance(x, tuple) else x
+
+    def regs(*xs):
+        out = []
+        for x in xs:
+            if isinstance(x, tuple):
+                out += x[1]
+        return out
+
+    def op(q, fn, outs, ins, grp=None, inc=16, dma=True, rate=None, **more):
+        o = {"q": q, "fn": fn, "w": regs(*outs), "r": regs(*ins), "grp": grp, "inc": inc, "dma": dma,
+             "part": any(x[2] for x in outs), "hold": 0.0, "late": 0.0}
+        big = [x for x in ins if isinstance(x, tuple) and x[3] != 1]
+        if grp is not None:
+            o["hold"], o["late"] = (100.0, 2500.0) if dma else (500.0 if q else 0.0, 3000.0 if q else 500.0)
+        elif q == "P":
+            o["hold"], o["late"] = 10 + 0.52 * max(64, outs[0][3]) * (4 if ins[0][4] == F32 else 1), 140.0
+        elif q == "G":
+            o["hold"] = 130 + 2.08 * outs[0][3]
+        else:
+            o["gn"] = outs[0][3] if any(x[3] == 0 for x in big) else 0
+            if o["gn"]:
+                rate = TUNE["gather"]
+            elif rate is None:
+                rate = 0.5 if q == "V" and all(x[4] in (BF, U16) for x in big + [outs[0]]) else 1.0
+            o["hold"] = 55 + 1.04 * max(64, rate * outs[0][3])
+        o.update(more)
+        ops.append(o)
+
+    def tt(out, x, y, o):
+        op("V", lambda e: e.tensor_tensor(out[0], x[0], y[0], o), [out], [x, y],
+           rate=1.0 if "ps" in (x[1][0][0], y[1][0][0]) else 2.0)
+
+    def ts(out, x, s1, o0, s2=None, o1=None):
+        if o1 is None:
+            op("V", lambda e: e.tensor_scalar(out[0], x[0], val(s1), None, o0), [out], [x, s1])
+        else:
+            op("V", lambda e: e.tensor_scalar(out[0], x[0], val(s1), val(s2), o0, o1), [out], [x, s1, s2])
+
+    def cp(out, x):
+        op("V", lambda e: e.tensor_copy(out[0], x[0]), [out], [x])
+
+    def ms(out, c):
+        op("V", lambda e: e.memset(out[0], c), [out], [])
+
+    def scan(out, d0, d1, o0, o1):
+        op("V", lambda e: e.tensor_tensor_scan(out[0], d0[0], d1[0], 0.0, o0, o1), [out], [d0, d1])
+
+    def act(out, x, f=AF.Identity, bias=0.0, scale=1.0, acc=None):
+        if acc is None:
+            op("S", lambda e: e.activation(out[0], x[0], f, bias=val(bias), scale=val(scale)), [out], [x, bias, scale])
+        else:
+            op("S", lambda e: e.activation(out[0], x[0], f, bias=val(bias), scale=val(scale), accum_out=acc[0]), [out, acc], [x, bias, scale])
+
+    def mm(out, l, r, start, stop, **more):
+        op("P", lambda e: e.matmul(out[0], l[0], r[0], start, stop), [out], [l, r], **more)
+
+    def mmg(items):
+        for j, (out, l, r) in enumerate(items):
+            mm(out, l, r, j == 0, j == len(items) - 1, join=j > 0)
+
+    def iota(out, pat, base=0, cm=0, small=True):
+        if small:
+            op("G", lambda e: e.iota(out[0], pat, base, cm, allow_small_or_imprecise_dtypes=True), [out], [])
+        else:
+            op("G", lambda e: e.iota(out[0], pat, base, cm), [out], [])
+
+    def dma(q, grp, out, x, kb=60):
+        op(q, lambda e: e.dma_start(out[0], x[0]), [out], [x], grp, move=3.4 * kb)
+
+    def masks(src, dsts):
+        sets = [topo.engines(src, d) for d in dsts]
+        narrow = min(sets, key=len)
+        tight = [j for j, s in enumerate(sets) if len(s) == len(narrow)]
+        wide = [j for j in range(len(dsts)) if j not in tight]
+        out = {}
+        for group, pool in ((tight, narrow), (wide, [e for e in max(sets, key=len) if e not in narrow])):
+            if group:
+                n = 1
+                while 2 * n * len(group) <= len(pool):
+                    n *= 2
+                for i, j in enumerate(group):
+                    out[j] = pool[i * n:(i + 1) * n]
+        return [out[j] for j in range(len(dsts))]
+
+    def exchange(tag, sign, srcs, dsts):
+        to = [T.cores[(rank + sign * (1 + d)) % N] for d in range(N - 1)]
+        eng = masks(core, to)
+        tr = []
+        for d in range(N - 1):
+            rid, pid, _ = topo.addr(to[d])
+            tr.append(RemoteDMATransfer(dst_ids=[DstId(rid=rid, pnc=pid)], dma_engine_mask=sum(1 << e for e in eng[d]),
+                                        remote_sem=T.sem["arr%d" % tag], src=srcs[d][0], dst=dsts[d][0]))
+        op("G", lambda e: e.remote_dma_fused(tr, local_sem=T.sem["snd%d" % tag]), [], srcs, "snd%d" % tag, sum(len(x) for x in eng), False)
+        got = 0
+        for d in range(N - 1):
+            r = (rank - sign * (1 + d)) % N
+            got += len(masks(T.cores[r], [T.cores[(r + sign * (1 + k)) % N] for k in range(N - 1)])[d])
+        op(None, None, dsts, [], "arr%d" % tag, got, False)
+
+    R0, R1, R8 = slice(0, 128, 16), slice(1, 128, 16), slice(0, 8)
+    col = lambda j: a("col", j, j + 1)
+    mat = lambda j: a("mats", 128 * j, 128 * (j + 1))
+    sel = lambda name, j: a(name, 128 * j, 128 * (j + 1))
+    NEG, B2, BN, EP, EN, HALF = range(6)
+    PM, PG, PP, H0, H1, SC0, SC1, BA0, BA1, BB0, BB1, FS0, FS1, FB0, FB1, L01 = range(16)
+    CD, CF, CQ, CG, CI = 0, 512, 640, 896, 1024
+    one = a("lc", p=slice(0, 1))
+    row = lambda lo, n: a("cv", lo, lo + n, p=slice(0, 1))
+    xt = lambda t, *k: a("xt%d" % (t % 2), *k)
+    wn = lambda t, *k: a("wn%d" % (t % 2), *k)
+    ot = lambda t, *k, **kw: a("ot%d" % (t % 2), *k, **kw)
+    half = lambda name, t, lo=0, hi=256: a(name, 256 * (t % 2) + lo, 256 * (t % 2) + hi)
+    slot = lambda name, t, lo=0, hi=256: a(name, 256 * t + lo, 256 * t + hi)
+    lanes = lambda name, m: a(name, m, NV, ST)
+    ch = lambda name, c: a(name, 1024 * c, 1024 * (c + 1))
+    pair = [0]
+    pair_of = {}
+    pp = lambda key: a("ps", pair_of[key], pair_of[key] + 1024)
+    PD, XV, P2, P3 = a("ps", 3072, 3328), a("ps", 3328, 3584), a("ps", 3584, 3840), a("ps", 3840, 4096)
+    PA, PGO = a("ps", 3900, 3901), a("ps", 3840, 3888)
+    yv = a("s3", 15, 4096, 16)
+
+    dma("Y", "lf", a("fst"), hbm(T.f0[:]))
+    for j in range(4):
+        dma("Y", "lk%d" % j, a("ktb", 768 * j, 768 * (j + 1)), hbm(T.kt[:, 768 * j:768 * (j + 1)]), 390)
+    dma("Y", "lxg", a("xt0", NV, NW), hbm(T.x0[:, NV:NW]), 200)
+    dma("Y", "lt", a("thi"), hbm(T.th[:]))
+    dma("Y", "ls", a("shi"), hbm(T.shw[:]))
+    dma("Y", "lx0", a("xt0", 0, NV), hbm(T.x0[:, 0:NV]), 790)
+    dma("Y", "lx1", a("xt1", 0, NV), hbm(T.x0[:, 0:NV]), 790)
+
+    iota(a("pi", 0, 1), [[0, 1]], 0, 1, False)
+    iota(a("qg"), [[1, 8], [0, 16]])
+    iota(a("q128"), [[1, 128]])
+    iota(a("cv", CI, CI + 256), [[1, 256]])
+    iota(a("bas"), [[16, 48]], 256)
+    ts(a("pi", 1, 2), a("pi", 0, 1), 15, OP.bitwise_and)
+    ts(a("pi", 2, 3), a("pi", 0, 1), 4, OP.arith_shift_right)
+    ms(a("gt", NV, NW), 16.0 * S)
+    cp(col(PM), a("pi", 1, 2))
+    cp(col(PG), a("pi", 2, 3))
+    cp(col(PP), a("pi", 0, 1))
+    ts(col(H0), col(PM), 7.5, OP.is_lt)
+    ts(col(H1), col(PM), 7.5, OP.is_gt)
+    ts(a("blk"), a("qg"), col(PG), OP.is_equal)
+    ts(a("m16"), a("q128", 0, 16), col(PM), OP.is_equal)
+    ts(a("col", FS0, FS1 + 1), a("col", H0, H1 + 1), 64.0, OP.mult)
+    ts(a("col", FB0, FB1 + 1), a("col", H0, H1 + 1), 16.0, OP.mult)
+    tt(a("m8"), a("m16", 0, 8), a("m16", 8, 16), OP.add)
+    ts(a("col", SC0, SC1 + 1), a("col", H0, H1 + 1), 1.0 / S, OP.mult)
+    ts(a("col", BA0, BA1 + 1), a("col", H0, H1 + 1), 239.0625, OP.mult, 0.46875, OP.add)
+    ts(a("col", BB0, BB1 + 1), a("col", H0, H1 + 1), 479.53125, OP.mult, -240.0, OP.add)
+    for j in range(8):
+        ts(sel("sw2", j), a("blk"), a("m8", j, j + 1), OP.mult, float(S), OP.mult)
+    for h in range(2):
+        ts(a("f2", 192 * h, 192 * (h + 1)), a("fst"), col(FS0 + h), OP.mult, col(FB0 + h), OP.add)
+    for j in range(8):
+        mm(a("ps", 512 * j, 512 * j + 384), sel("sw2", j), a("f2"), True, True)
+    ts(a("eye"), a("q128"), col(PP), OP.is_equal)
+    ms(a("lc", p=slice(0, 64)), 0.0)
+    ms(a("cv", CD, CD + 512, p=slice(0, 32)), 0.0)
+    ms(a("cv", CD, CD + 512, p=slice(32, 64)), 1.0 / 32)
+    ms(a("cv", CF, CF + 128), -768.0 * S * 512)
+    ts(mat(NEG), a("eye"), -1.0, OP.mult)
+    ms(a("lc", p=slice(0, 1)), 1.0)
+    ms(a("lc", p=slice(32, 33)), 1.0)
+    ms(a("cv", CD + 15, CD + 512, 16, p=slice(0, 32)), -80.0 * S)
+    ms(a("cv", CD + 15, CD + 512, 16, p=slice(32, 64)), -15.0 / 32)
+    ts(a("col", 16, 32), a("m16"), -2048.0, OP.mult)
+    for k in range(16):
+        act(sel("dga", k), a("eye"), scale=col(16 + k))
+    ts(col(L01), col(PM), 1.5, OP.is_lt)
+    iota(a("slo"), [[0, 2048]])
+    ts(a("b01"), a("blk"), col(L01), OP.mult)
+    for j in range(8):
+        act(sel("sw3", j), sel("sw2", j), scale=17.0 / S)
+    for k in range(16):
+        act(a("slo", 128 * k + k, 128 * (k + 1), 16), a("b01", k, 128, 16))
+    act(a("dgb"), a("dga"), scale=-128.0)
+    for j, src, c in ((B2, "blk", 2.0), (BN, "blk", -1.0), (EP, "eye", 2.0 ** -18), (EN, "eye", -2.0 ** -18), (HALF, "eye", 0.5)):
+        act(mat(j), a(src), scale=c)
+    iota(a("va"), [[192, 16], [0, 16]])
+    iota(a("vb"), [[1, 3], [0, 16], [12, 16]])
+    exchange(RO, 1, [a("xt0", NV + 256 * d, NV + 256 * (d + 1)) for d in range(3)],
+             [a("wn0", 256 * (d + 1), 256 * (d + 2)) for d in range(3)])
+    iota(a("vt"), [[1, 2], [12, 256]])
+
+    def late_constants():
+        ms(a("cv", CQ, CQ + 256), -0.25)
+        ms(a("cv", CG, CG + 48), 130048.0)
+        iota(a("rs3"), [[0, 1024]], 1)
+        iota(a("rs5"), [[0, 768]], 1)
+        ms(a("rs3", 0, 1024, 16), 0.0)
+        ms(a("rs5", 0, 768, 256), 0.0)
+        for name in ("ot0", "ot1"):
+            for lo in range(0, 4352, 1088):
+                iota(a(name, lo, lo + 1088), [[0, 1088]])
+        ts(a("thm"), a("qg"), col(PP), OP.is_equal, -1.0, OP.mult)
+        ts(a("cnm"), a("q128"), 0.0, OP.mult, a("m16", 0, 1), OP.add)
+        ts(a("bas"), a("bas"), col(PM), OP.add)
+        cp(a("ffl"), a("fst"))
+        dma("Y", "dff", a("ff", p=R0), a("ffl"))
+        dma("Y", "dva", a("ot0", 0, 256, p=R0), a("va", p=R0))
+        dma("Y", "dva", a("ot1", 0, 256, p=R0), a("va", p=R0))
+        cp(a("thc"), a("thi"))
+        dma("Y", "dth", a("thf", p=R8), a("thc"), 30)
+        cp(a("shu"), a("shi"))
+
+    def entries(t, src, off):
+        ts(a("ci"), src, S - 1, OP.bitwise_and)
+        ts(half("own", t), src, 1.0 / 32 - off, OP.add)
+        cp(half("c16", t), a("ci"))
+        for h in range(2):
+            act(a("w2a", 512 * (t % 2) + h, 512 * (t % 2 + 1), 2), half("own", t), bias=col(BA0 + h), scale=col(SC0 + h))
+
+    def gat_f(t, c, on_vector=False):
+        (cp if on_vector else act)(ch("fg", c), ind(a("gt"), half("o16", t - 3, 64 * c, 64 * (c + 1))))
+
+    def give_back(t):
+        lo = 1024 * ((pair[0] + 2) % 3) + 512
+        PF, PT = a("ps", lo, lo + 256), a("ps", lo + 256, lo + 512)
+        for c in range(4):
+            mmg([(a("ps", lo + 64 * c, lo + 64 * (c + 1)), sel("dga", k), a("fg", 1024 * c + k, 1024 * (c + 1), 16)) for k in range(16)])
+        ts(PF, PF, -900000.0 * 512, OP.is_gt, -1.0, OP.mult)
+        tt(PT, half("dkm", t - 3), PF, OP.mult)
+        tt(lanes("gt", t % 3), lanes("gt", t % 3), PT, OP.add)
+        tt(a("kin"), slot("kp", t - 3), PT, OP.add)
+        act(half("frn", t - 3), PF)
+        entries(t, a("kin"), 16.0 * S)
+
+    def weights(key, name, rhs, base, c):
+        pair_of[key] = 1024 * (pair[0] % 3)
+        pair[0] += 1
+        for b in range(2):
+            lo = pair_of[key] + 512 * b
+            for j in range(8):
+                mm(a("ps", lo + j, lo + 512, 8), sel(name, j), a(rhs, base + 128 * c + 64 * b, base + 128 * c + 64 * (b + 1)),
+                   True, True, join=j > 0)
+
+    w2 = lambda t, c: weights(("a", t, c), "sw2", "w2a", 512 * (t % 2), c)
+    w3 = lambda t, c: weights(("b", t, c), "sw3", "w2b", 0, c)
+
+    def gat_g(t, c):
+        (cp if (TUNE["gv"] >> t) & 1 and c == 1 else act)(ch("gg", c), ind(a("gt"), half("c16", t, 64 * c, 64 * (c + 1))))
+
+    def zr(t, c):
+        tt(ch("zz", c), ch("gg", c), pp(("a", t, c)), OP.subtract)
+        if (TUNE["rs"] >> (4 * t + c)) & 1:
+            act(ch("rr", c), ch("zz", c), AF.Relu, bias=160.0 * S)
+        else:
+            ts(ch("rr", c), ch("zz", c), -160.0 * S, OP.max, 160.0 * S, OP.add)
+        for b in range(2):
+            lo, x = pair_of[("a", t, c)] + 512 * b, 1024 * c + 512 * b
+            mmg([(a("ps", lo, lo + 512), a("lc", p=slice(0, 33)), a("cv", CD, CD + 512, p=slice(0, 33))),
+                 (a("ps", lo, lo + 512), mat(NEG), a("rr", x, x + 512)),
+                 (a("ps", lo, lo + 511), a("eye"), a("rr", x + 1, x + 512)),
+                 (a("ps", lo + 15, lo + 511, 16), mat(NEG), a("rr", x + 16, x + 512, 16))])
+
+    def scan2(t, c):
+        scan(ch("so", c), ch("gg", c), pp(("a", t, c)), OP.max, OP.add)
+
+    def flag(h):
+        out = a("ps", 3072 + 128 * h, 3072 + 128 * (h + 1))
+        mmg([(out, one, row(CF, 128))] + [(out, sel("dga", k), a("zz", 2048 * h + k, 2048 * (h + 1), 16)) for k in range(16)])
+
+    def own_key(t, h):
+        tt(a("ps", 3328 + 128 * h, 3328 + 128 * (h + 1)), half("own", t, 128 * h, 128 * (h + 1)),
+           a("ps", 3072 + 128 * h, 3072 + 128 * (h + 1)), OP.min)
+
+    def winners(t, h):
+        lo, hi = 128 * h, 128 * (h + 1)
+        b = a("ps", 3584 + lo, 3584 + hi)
+        tt(b, a("so", 2048 * h + 15, 2048 * (h + 1), 16), a("ps", 3328 + lo, 3328 + hi), OP.max)
+        ts(slot("kp", t, lo, hi), b, 16.0 * S, OP.add)
+        tt(a("fra", lo, hi), b, slot("kp", t, lo, hi), OP.subtract)
+        if t < 2:
+            tt(half("dkn", t, lo, hi), b, a("ktb", t + ST * lo, ST * hi, ST), OP.subtract)
+        for j in range(2):
+            act(a("w2b", 2 * lo + j, 2 * hi, 2), b, bias=col(BB0 + j), scale=col(SC0 + j))
+        ts(a("cj", lo, hi), slot("kp", t, lo, hi), S - 1, OP.bitwise_and)
+        cp(a("d16", lo, hi), a("cj", lo, hi))
+
+    def gat_x(t, c):
+        act(ch("xg", c), ind(xt(t), a("d16", 64 * c, 64 * (c + 1))))
+
+    def min3(t, c):
+        tt(ch("t3", c), ch("xg", c), pp(("b", t, c)), OP.min)
+
+    def scan3(c):
+        scan(ch("s3", c), a("rs3"), ch("t3", c), OP.mult, OP.max)
+
+    def status(t):
+        m = t % 3
+        xv = xt(t, m, NV, ST)
+        mm(XV, a("eye"), xv, True, True)
+        mm(PD, a("thm", p=R8), a("thf", 256 * m, 256 * (m + 1), p=R8), True, False, lock=[("ps", 3072, 3584)])
+        mm(PD, mat(BN), xv, False, False, join=True)
+        tt(a("mxv"), yv, XV, OP.max)
+        mm(PD, mat(BN), yv, False, False, lock=[("ps", 3072, 3584)])
+        mm(PD, mat(B2), a("mxv"), False, True, join=True)
+        mmg([(P2, mat(EN), xv), (P2, mat(EP), yv)])
+        act(a("yc"), yv)
+        last = t == RO - 1
+        ts(slot("fd", t) if last else PD, PD, 0.0 if t == 0 else a("am", 0, 1), OP.is_lt, 64.0 * S, OP.mult)
+        if not last:
+            tt(lanes("gt", m), slot("kp", t), PD, OP.add)
+            act(slot("fd", t), PD)
+
+    def new_x(t):
+        m = t % 3
+        xv = xt(t, m, NV, ST)
+        tt(a("tt4"), slot("fd", t), P2, OP.mult)
+        mmg([(P3, one, row(CQ, 256)), (P3, mat(HALF), xv), (P3, mat(HALF), a("yc")), (P3, mat(HALF), a("tt4"))])
+        ts(wn(t, 0, 256), P3, 1.5 * 2 ** 23, OP.add, -1.5 * 2 ** 23, OP.add)
+        tt(a("ne"), wn(t, 0, 256), XV, OP.not_equal)
+        mm(P2, a("blk"), a("ne"), True, True)
+        cp(xt(t + 1, m, NV, ST), wn(t, 0, 256))
+        act(a("chs"), P2, AF.Sign, scale=-1.0)
+        if t < RO - 1:
+            act(xt(t, m, NV, ST), wn(t, 0, 256))
+
+    def count_changes(t):
+        old = a("fo") if t < 3 else slot("fd", t - 3)
+        mmg([(P2, a("eye"), slot("fd", t)), (P2, mat(NEG), old)])
+        act(a("ab"), P2, AF.Abs, scale=2.0 ** -18, acc=a("cnt", 0, 1))
+        mm(PA, a("cnm"), a("cnt", 0, 1), True, True)
+        ts(a("qi", 0, 1), PA, -31.5, OP.add, 1.0 / 64, OP.mult)
+        ts(a("am", 0, 1), a("qi", 0, 1), -64.0, OP.mult, PA, OP.add)
+
+    def old_status(t):
+        ts(a("fo"), lanes("gt", t % 3), 200000.0, OP.is_gt, 64.0 * S, OP.mult)
+
+    def final_status(t):
+        act(lanes("ff", t % 3), slot("fd", t), scale=2.0 ** -18)
+
+    def gat2(out, base, win, off, split):
+        if split:
+            cp(a(out, base, base + 384), ind(win, a(off, 0, 24)))
+            act(a(out, base + 384, base + 768), ind(win, a(off, 24, 48)))
+        else:
+            act(a(out, base, base + 768), ind(win, a(off)))
+
+    def ghosts(t):
+        last = t == RO - 1
+        gat2("hh", 0, a("chs"), "shu", last)
+        scan(a("cum"), a("rs5"), a("hh"), OP.mult, OP.add)
+        mmg([(PGO, one, row(CG, 48))] + [(PGO, sel("dgb", k), a("hh", k, 768, 16)) for k in range(16)] +
+            [(PGO, sel("dga", k), a("cum", k, 768, 16)) for k in range(16)])
+        tt(a("q48"), a("bas"), PGO, OP.min)
+        tt(a("r48"), a("q48"), a("shi"), OP.max)
+        cp(a("o48"), a("r48"))
+        gat2("wn%d" % ((t + 1) % 2), 256, wn(t), "o48", last)
+        exchange(t, -1, [wn(t + 1, 256 * (d + 1), 256 * (d + 2)) for d in range(3)],
+                 [xt(t + 1, NV + 256 * d, NV + 256 * (d + 1)) for d in range(3)])
+
+    def origin_table(t):
+        cp(a("chi"), a("ci"))
+        mm(P3, a("eye"), a("chi"), True, True)
+        tt(a("clo"), a("ci"), P3, OP.subtract)
+        m = t % 3
+        dma("Y", "ot_%d" % t, ot(t, 256, 4352, p=R0), a("chi"))
+        dma("Y", "ot_%d" % t, ot(t, 256, 4352, p=R1), a("clo"))
+        dma("Y", "ot_%d" % t, ot(t, 0, 256, p=R1), a("vb", 256 * m, 256 * (m + 1), p=R1))
+
+    def origin_place(t):
+        act(half("kb", t), a("fra"), bias=256.0 - 2.0 ** 29, scale=-8192.0)
+        mmg([(P3, one, row(CI, 256)), (P3, a("eye"), half("kb", t))])
+        cp(half("oo", t), P3)
+
+    def gat_o(t, c):
+        act(ch("og", c), ind(ot(t), half("oo", t, 64 * c, 64 * (c + 1))))
+
+    def origins(t):
+        mmg([(P3, sel("slo", k), a("og", k, 4096, 16)) for k in range(16)])
+        if t < 2:
+            cp(half("o16", t), P3)
+            tt(half("dov", t), P3, half("vt", t), OP.subtract)
+            ts(P3, half("dov", t), 0.0, OP.not_equal)
+            tt(half("dkm", t), half("dkn", t), P3, OP.mult)
+        elif t == 2:
+            act(a("yob"), P3)
+        else:
+            tt(a("yob"), a("yob"), P3, OP.add)
+
+    def kept_origin(t):
+        tt(P2, half("kb", t), half("frn", t - 3), OP.is_equal)
+        tt(P2, half("dov", t - 3), P2, OP.mult)
+        tt(a("yob"), a("yob"), P2, OP.add)
+
+    for q in range(16):
+        j, h = q % 8, q // 8
+        if q == 12:
+            entries(0, lanes("ktb", 0), 0.0)
+        tt(a("gt", 192 * q, 192 * (q + 1)), a("ktb", 192 * q, 192 * (q + 1)), a("ps", 512 * j + 192 * h, 512 * j + 192 * (h + 1)), OP.add)
+    w2(0, 0), w2(0, 1), w2(0, 2)
+
+    for t in range(RO):
+        u = t - 1
+        if t >= 3:
+            gat_f(t, 0), gat_f(t, 1, TUNE["fv"] > 1), gat_f(t, 2), gat_f(t, 3, TUNE["fv"] > 0)
+            new_x(u)
+            give_back(t)
+            w2(t, 0), w2(t, 1), w2(t, 2)
+            ghosts(u)
+            origin_table(t)
+        elif t > 0:
+            new_x(u)
+            ghosts(u)
+        else:
+            late_constants()
+            origin_table(0)
+        for c in range(4):
+            gat_g(t, c)
+        zr(t, 0)
+        zr(t, 1)
+        flag(0)
+        if t > 0:
+            count_changes(u)
+        scan2(t, 0)
+        w2(t, 3)
+        own_key(t, 0)
+        scan2(t, 1)
+        winners(t, 0)
+        w3(t, 0)
+        gat_x(t, 0), gat_x(t, 1)
+        zr(t, 2)
+        zr(t, 3)
+        flag(1)
+        scan2(t, 2)
+        w3(t, 1)
+        own_key(t, 1)
+        scan2(t, 3)
+        winners(t, 1)
+        origin_place(t)
+        w3(t, 2)
+        gat_x(t, 2), gat_x(t, 3)
+        min3(t, 0)
+        w3(t, 3)
+        min3(t, 1)
+        scan3(0)
+        scan3(1)
+        if t < 3:
+            old_status(t)
+        if t < 2:
+            entries(t + 1, lanes("ktb", t + 1), 0.0)
+        if t == 3:
+            tt(a("ykb"), slot("kp", 2), slot("kp", 3), OP.add)
+            act(a("yka"), a("ykb"), bias=-48.0 * S)
+        if t == 4:
+            kept_origin(3)
+            tt(a("ykb"), a("yka"), slot("kp", 4), OP.add)
+            dma("Y", "oyk", hbm(T.yk[:]), a("ykb"))
+        if t > 0:
+            for c in range(4):
+                gat_o(u, c)
+        if t < 2:
+            origin_table(t + 1)
+        min3(t, 2)
+        if t < 2:
+            w2(t + 1, 0)
+        scan3(2)
+        min3(t, 3)
+        if t < 2:
+            w2(t + 1, 1), w2(t + 1, 2)
+        scan3(3)
+        if t > 0:
+            origins(u)
+        status(t)
+        if t >= 2:
+            final_status(t)
+    t = RO - 1
+    dma("Y", "oyf", hbm(T.yf[:]), a("ff", p=R0))
+    new_x(t)
+    dma("Y", "oyx", hbm(T.yx[:, 0:NV]), xt(t + 1, 0, NV), 790)
+    ghosts(t)
+    for c in range(4):
+        gat_o(t, c)
+    kept_origin(t)
+    origins(t)
+    dma("Y", "oyo", hbm(T.yo[:]), a("yob"))
+    dma("S", "oyg", hbm(T.yx[:, NV:NW]), xt(t + 1, NV, NW), 200)
+    ops.append({"q": "Y", "fn": None, "w": [], "r": [], "grp": None, "final": True, "hold": 0.0, "late": 0.0})
+    _emit(g, T, _arrange(ops))

@@ -3,7 +3,9 @@ from concourse.mybir import AluOpType as OP, ActivationFunctionType as AF
 
 N, NV, NW, NL, ST, RO = 4, 3072, 3840, 256, 12, 5
 S = 4096
-F32, BF, I32, U16 = "float32", "bfloat16", "int32", "uint16"
+BIG = 2.0 ** 24
+CUTS = (0, 4, 8, 12, 15, 16)
+F32, BF, I32, U16, F16 = "float32", "bfloat16", "int32", "uint16", "float16"
 
 
 def _sb(n, d):
@@ -13,40 +15,65 @@ def _sb(n, d):
 SCRATCH = {
     "ps": ("psum", [128, 4096], F32),
     "ktb": _sb(NV, I32), "gt": _sb(NW, F32), "xt0": _sb(NW, BF), "xt1": _sb(NW, BF),
-    "fst": _sb(192, I32), "f2": _sb(384, BF), "ffl": _sb(192, F32), "ff": _sb(NV, F32),
-    "thi": _sb(48, I32), "thc": _sb(48, F32), "thf": _sb(768, F32), "shi": _sb(48, I32), "shu": _sb(48, U16),
+    "fst": _sb(192, I32), "f2": _sb(384, BF), "ffl": _sb(192, F32), "ff": _sb(NV, F32), "fb": _sb(192, BF), "f8": _sb(NV, BF),
+    "thi": _sb(48, I32), "thc": _sb(48, F16), "thf": _sb(768, F16), "shi": _sb(48, I32), "shu": _sb(48, U16),
     "gg": _sb(4096, F32), "zz": _sb(4096, BF), "rr": _sb(4096, BF), "so": _sb(4096, F32),
-    "xg": _sb(4096, BF), "og": _sb(4096, BF), "ot0": _sb(4352, BF), "ot1": _sb(4352, BF),
-    "pi": _sb(4, I32), "col": _sb(32, F32), "q128": _sb(128, F32), "qg": _sb(128, F32), "m16": _sb(16, F32), "m8": _sb(8, F32),
-    "eye": _sb(128, BF), "blk": _sb(128, BF), "b01": _sb(128, BF), "mats": _sb(6 * 128, BF),
-    "sw2": _sb(1024, BF), "sw3": _sb(1024, BF), "dga": _sb(2048, BF), "dgb": _sb(2048, BF), "slo": _sb(2048, BF),
-    "thm": _sb(128, F32), "cnm": _sb(128, F32), "lc": _sb(128, BF), "cv": _sb(1280, BF),
-    "rs3": _sb(1024, BF), "rs5": _sb(768, BF), "va": _sb(256, BF), "vb": _sb(768, BF), "vt": _sb(512, F32), "bas": _sb(48, F32),
-    "ci": _sb(256, I32), "c16": _sb(512, U16), "own": _sb(512, F32), "w2a": _sb(1024, BF), "w2b": _sb(512, BF),
-    "chi": _sb(256, BF), "clo": _sb(256, BF), "kp": _sb(5 * 256, I32), "kin": _sb(256, I32),
-    "cj": _sb(256, I32), "d16": _sb(256, U16), "fd": _sb(5 * 256, BF), "fo": _sb(256, BF),
-    "mxv": _sb(256, BF), "tt4": _sb(256, BF), "yc": _sb(256, BF), "wn0": _sb(1024, BF), "wn1": _sb(1024, BF),
-    "ne": _sb(256, BF), "chs": _sb(256, BF), "hh": _sb(768, BF), "cum": _sb(768, BF),
-    "q48": _sb(48, F32), "r48": _sb(48, F32), "o48": _sb(48, U16),
+    "xg": _sb(4096, BF), "t3": _sb(4096, BF), "s3": _sb(4096, BF), "so2": _sb(2048, F32),
+    "pi": _sb(4, I32), "col": _sb(16, F32), "q128": _sb(128, F32), "qg": _sb(128, F32), "m16": _sb(17, F32), "m8": _sb(8, F32),
+    "rev": _sb(8, F32), "c8": _sb(16, F32), "r8": _sb(24, BF), "md": _sb(16, F32), "thm": _sb(128, BF), "bks": _sb(128, BF),
+    "eye": _sb(128, BF), "blk": _sb(128, BF), "b17": _sb(128, BF), "bs16": _sb(48, F16), "mats": _sb(9 * 128, BF),
+    "sw2": _sb(1024, BF), "sw3": _sb(1024, BF), "dgd": _sb(17 * 128, BF), "csel": _sb(1024, BF),
+    "cnm": _sb(128, F32), "lc": _sb(384, BF), "cv": _sb(1536, BF), "vv": _sb(768, BF),
+    "rs2": _sb(1024, BF), "rs3": _sb(1024, BF), "cap": _sb(256, BF), "bas": _sb(48, F32), "zt": _sb(256, BF),
+    "ci": _sb(768, I32), "c16": _sb(5 * 256, U16), "cf": _sb(5 * 256, F16), "kf": _sb(5 * 256, F32), "w2a": _sb(5 * 512, BF),
+    "w2b": _sb(512, BF), "kp": _sb(5 * 256, I32), "kin": _sb(256, I32), "t1": _sb(256, F32),
+    "cj": _sb(256, I32), "d16": _sb(256, U16), "fra": _sb(256, F32), "uu": _sb(256, BF),
+    "xa": _sb(256, F32), "x1": _sb(256, F32), "x3": _sb(256, I32), "og": _sb(5 * 256, I32), "o16": _sb(512, U16), "of": _sb(512, F16),
+    "ne": _sb(512, BF), "rs": _sb(512, BF), "fs": _sb(5 * 256, BF), "ad": _sb(256, BF), "ae": _sb(256, BF),
+    "tt4": _sb(256, BF), "wn0": _sb(1024, BF), "wn1": _sb(1024, BF), "chs": _sb(256, BF), "hh": _sb(768, BF), "cum": _sb(768, BF),
+    "r48": _sb(48, F32), "o48": _sb(48, U16),
     "ab": _sb(256, BF), "cnt": _sb(4, F32), "qi": _sb(4, I32), "am": _sb(4, F32),
-    "fra": _sb(256, F32), "kb": _sb(512, BF), "oo": _sb(512, U16), "o16": _sb(512, U16), "dov": _sb(512, F32),
-    "dkn": _sb(512, I32), "dkm": _sb(512, F32), "frn": _sb(512, BF),
-    "yob": _sb(256, F32), "ykb": _sb(256, F32), "yka": _sb(256, F32),
+    "yob": _sb(256, F32), "yoa": _sb(256, F32), "ykb": _sb(256, F32), "yka": _sb(256, F32),
 }
-ALIAS = {"fg": "xg", "t3": "zz", "s3": "rr"}
-DMA_GROUPS = ["lf", "lk0", "lk1", "lk2", "lk3", "lt", "ls", "lxg", "lx0", "lx1", "dff", "dva", "dth", "ot_0", "ot_1", "ot_2", "ot_3", "ot_4",
-              "oyx", "oyg", "oyf", "oyk", "oyo"]
+DMA_GROUPS = ["lf", "lk0", "lk1", "lk2", "lk3", "lk4", "lt", "ls", "lxg", "lx0", "lx1", "dff", "df8", "dth", "oyx", "oyg", "oyf", "oyk", "oyo"]
 SEMAPHORES = (["eV", "eS", "eP", "eG"] + DMA_GROUPS + ["snd%d" % t for t in range(RO + 1)] + ["arr%d" % t for t in range(RO + 1)])
 
-TUNE = {"look": 200.0, "alpha": 3.0, "gather": 1.56, "fv": 2, "gv": 24, "rs": 0}
-ORDER = [
-17,10,15,16,18,19,0,21,22,11,12,24,20,26,27,59,23,25,38,33,40,39,48,49,34,44,50,35,31,32,37,81,85,29,74,70,149,86,106,1,117,2,3,4,5,8,6,53,36,28,42,115,41,114,45,118,75,73,63,71,80,7,62,65,64,9,144,150,143,148,147,113,109,110,151,160,161,46,119,121,43,116,123,125,122,124,47,120,127,132,79,72,129,130,131,139,126,133,134,135,137,136,138,140,77,111,128,51,54,145,165,166,52,55,236,57,56,171,175,58,176,178,177,14,154,162,163,172,153,179,180,181,182,173,201,202,203,68,174,61,66,67,168,170,247,184,186,185,69,83,60,183,107,103,105,82,188,205,209,167,141,237,155,206,169,187,189,30,190,192,195,213,196,112,84,193,194,204,210,208,207,214,191,215,216,242,221,217,222,13,152,245,199,197,198,230,200,212,211,233,234,219,220,227,228,226,248,235,251,232,258,231,259,229,252,257,157,260,104,261,238,218,108,223,224,263,262,240,241,249,250,264,265,239,225,158,156,243,244,246,255,254,253,256,266,267,268,284,288,142,289,291,269,76,270,271,290,285,292,296,286,273,363,164,319,275,297,298,287,146,320,322,362,305,355,276,277,302,304,303,293,295,278,356,279,78,280,281,361,88,91,323,299,300,294,324,306,364,307,272,308,357,313,311,101,90,89,93,360,98,312,282,283,354,314,321,328,317,318,325,326,332,327,331,309,333,301,310,334,336,339,335,337,99,315,316,348,385,330,386,338,345,92,341,102,95,342,329,350,340,352,343,365,159,367,369,351,366,100,87,94,97,96,344,346,370,353,368,347,349,374,373,379,387,380,381,382,358,274,359,372,371,376,388,391,392,389,375,481,480,383,384,393,394,377,378,390,395,396,397,398,411,415,416,400,412,424,402,418,417,425,426,399,419,403,404,420,421,429,431,430,422,423,405,406,427,407,413,445,414,449,408,409,410,446,447,450,452,483,482,549,433,432,428,434,435,439,436,437,438,440,451,458,448,454,453,457,459,460,461,464,442,456,441,443,473,465,493,444,455,476,462,466,463,469,467,468,474,475,470,478,472,486,477,471,484,488,620,622,487,485,494,495,496,479,497,499,500,504,516,503,515,506,518,505,490,489,501,507,491,492,498,517,519,520,522,621,523,401,508,509,525,527,528,510,511,513,535,524,521,526,550,544,551,547,552,530,531,563,534,529,533,536,532,537,512,554,555,556,557,538,558,559,545,562,539,553,623,686,568,570,569,560,561,540,584,588,592,541,542,543,585,587,586,589,591,590,572,564,514,571,546,573,574,578,579,575,596,576,577,565,580,581,593,597,598,630,582,612,599,603,600,604,595,594,583,615,601,602,609,613,566,617,616,610,608,624,567,625,614,631,611,605,626,627,635,502,606,607,634,632,548,618,619,633,636,637,640,642,628,629,638,761,760,643,655,652,641,644,653,654,656,657,659,662,664,660,665,645,646,647,648,650,672,661,658,663,688,681,684,669,667,700,666,670,668,671,673,674,687,691,692,694,693,695,696,697,698,675,676,705,706,707,690,651,639,689,701,677,678,762,763,679,680,699,721,722,649,724,725,729,723,726,709,727,728,708,710,733,711,715,716,713,714,718,682,717,730,732,734,683,735,712,736,740,741,770,702,703,737,704,719,749,731,771,720,752,738,739,745,746,751,747,764,685,742,743,744,750,768,753,765,748,766,754,767,755,772,773,756,757,774,800,775,799,798,776,779,769,780,781,782,783,785,788,758,759,784,786,787,789,790,791,792,793,794,801,805,777,778,802,803,804,806,807,795,796,797,808,809
-]
+TUNE = {"gather": 1.4, "hop": 40.0, "fv": {3: (1, 3), 4: (1, 3)}, "gv": {0: (1,)}, "xv": {},
+        "rs": {t: (2, 3) for t in range(RO)}, "dg": (), "eg": (1, 2),
+        "cv": ("c0", "c2", "c5", "c7", "c8", "c9", "c10", "c11")}
+PLAN = {
+    "V0": "c0 c2 c1 gt0 e00 gt1 gt2 e10 gt3 gt4 e20 e01 G1 Z0 e11 R0 c8 Z1 S0 R1 Z2 Z3 S1 b0 c9 kp0 cj0 c5 d0 fr0 c7 f20 S2 S3 "
+          "f11 b1 kp1 e21 cj1 f10 d1 M0 fr1 c11 M1 M2 T0 T1 M3",
+    "S0": "c4 c6 c14 e00 G0 e01 G2 G3 c3 zt0 c12 R2 wb0 R3 X0 uu0 f20 zt1 X1 wb1 X2 f10",
+    "P0": "c0 W0 W1 W2 A0 D0 A1 K0 W3 D1 A3 J0 A2 D2 D3 K1 J1",
+    "V1": "T2- T3- U0- U1- sc- gt- tt- x1- x2- wn- x4- Z0 cum- f21- R0 og- r48- o48- Z1 R1 c10- S0 Z2 Z3 qi- S1 am- b0 kp0 of- "
+          "cj0 d0 S2 fr0 S3 ne- b1 kp1 cj1 fr1 M0 d1 M1 T0 T1 M2 M3",
+    "S1": "X3- uu1- f11- c13- ad- ae- fs- xa- ch- G0 hh- G1 gw- G2 G3 ab- zt0 R2 R3 wb0 X0 zt1 X1 wb1 f21- uu0 X2",
+    "P1": "V0- V1- V2- P1- P0- V3- P3- P2- pd- pb- W0 pf- pc- k1- px- pn- W1 W2 A0 pg- D0 A1 D1 W3 K0 pa- A2 A3 J0 D2 D3 K1 pv- J1",
+    "V3": "T2- T3- U0- U1- sc- gt- tt- F1 F3 q0 x1- x2- wn- q1 cum- t1 t2 kin kf ci gb c16 x3- r48- x4- og- cf o48- qi- Z0 R0 Z1 "
+          "R1 S0 Z2 Z3 S1 am- b0 kp0 cj0 d0 S2 fr0 S3 b1 kp1 cj1 d1 M0 fr1 M1 T0 M2 T1 M3",
+    "S3": "X3- uu1- ad- ae- fs- xa- F0 ch- F2 hh- ab- rs wa G0 G1 gw- G2 G3 R2 zt0 R3 ff- wb0 X0 zt1 X1 wb1 uu0 X2",
+    "P3": "V0- V1- V2- P0- P1- V3- P3- P2- pd- pb- k1- pf- pc- px- k2- Q0 H0 Q1 pq H1 pn- pa- pg- p8- W0 W1 W2 A0 D0 A1 D1 W3 K0 "
+          "A2 A3 J0 D2 D3 K1 J1",
+    "V5": "T2- T3- U1- tt- yk-- hh- wn- cum- yk- r48- o48- gw- U0- sc- x1- x2- yo-- x3- x4- og- yo-",
+    "S5": "X3- uu1- ad- ae- fs- ch- hh- gw- ff- xa- end-",
+    "P5": "V0- V1- V2- P0- V3- P1- P2- P3- pd- pb- pc- px- pg- k1- p8- k2-",
+    "G0": "c0 c1 g3 e10 g5 g1 x e20 g2 g8 g4 g6 e11 e21 g7",
+    "N0": "x", "Y0": "load c7", "G5": "cp- gh-", "N5": "gh-", "Y5": "yk- yf- yx- yo- end-",
+}
+for _t in range(1, RO):
+    PLAN["G%d" % _t], PLAN["N%d" % _t] = "cp- gh- o16-", "gh-"
+for _q in "VSP":
+    PLAN[_q + "2"], PLAN[_q + "4"] = PLAN[_q + "1"], PLAN[_q + "3"]
 _ORDER = {}
 
 
+def _meet(x, y):
+    return x[1] < y[2] and y[1] < x[2] and x[4] < y[5] and y[4] < x[5] and (x[3] != y[3] or (x[1] - y[1]) % x[3] == 0)
+
+
 def _arrange(ops):
-    key = (len(ops), str(sorted(TUNE.items())))
+    key = (len(ops), str(sorted(TUNE.items())), str(PLAN))
     if key in _ORDER:
         return [ops[n] for n in _ORDER[key]]
     units, of = [], []
@@ -56,85 +83,55 @@ def _arrange(ops):
         else:
             units.append([n])
         of.append(len(units) - 1)
-    members = {}
-    for n, o in enumerate(ops):
-        if o["grp"] is not None:
-            members.setdefault(o["grp"], []).append(of[n])
+    sent = {o["grp"]: of[n] for n, o in enumerate(ops) if o["grp"] is not None}
     pred = [set() for _ in units]
     hist = {}
     for n, o in enumerate(ops):
         u = of[n]
-        for (regs, wr) in ((o["r"], False), (o["w"] + o.get("lock", []), True)):
-            for (name, lo, hi) in regs:
-                for (m, lo2, hi2, wr2) in hist.get(name, []):
-                    if (wr or wr2) and lo < hi2 and lo2 < hi:
-                        p = ops[m]
-                        if p["grp"] is None:
-                            pred[u].add(of[m])
-                        elif p["grp"] != o["grp"]:
-                            pred[u].update(members[p["grp"]])
-        if o["q"] is None:
-            pred[u].update(members["snd" + o["grp"][3:]])
+        for (regs, wr) in ((o["r"], False), (o["w"], True)):
+            for x in regs:
+                pred[u].update(of[m] for (m, y, wr2) in hist.get(x[0], []) if (wr or wr2) and _meet(x, y))
+        if o["q"] == "N":
+            pred[u].add(sent["snd" + o["grp"][3:]])
         if o.get("final"):
             pred[u].update(range(u))
         pred[u].discard(u)
-        for (regs, wr) in ((o["r"], False), (o["w"] + o.get("lock", []), True)):
-            for (name, lo, hi) in regs:
-                h = hist.setdefault(name, [])
+        for (regs, wr) in ((o["r"], False), (o["w"], True)):
+            for x in regs:
+                h = hist.setdefault(x[0], [])
                 if wr and not o.get("part"):
-                    h[:] = [e for e in h if not (lo <= e[1] and e[2] <= hi)]
-                h.append((n, lo, hi, wr))
+                    h[:] = [e for e in h if not (x[1] <= e[1][1] and e[1][2] <= x[2])]
+                h.append((n, x, wr))
     hold = [sum(ops[n]["hold"] for n in us) for us in units]
     late = [ops[us[-1]]["late"] for us in units]
+    move = [ops[us[0]].get("move", 0.0) for us in units]
     eng = [ops[us[0]]["q"] for us in units]
-    banks = [set(b for n in us for (name, lo, hi) in ops[n]["r"] + ops[n]["w"] if name == "ps" for b in range(lo // 512, (hi - 1) // 512 + 1))
+    banks = [set(b for n in us for x in ops[n]["r"] + ops[n]["w"] if x[0] == "ps" for b in range(x[1] // 512, (x[2] - 1) // 512 + 1))
              for us in units]
-    succ = [[] for _ in units]
-    for u, ps in enumerate(pred):
-        for p in ps:
-            succ[p].append(u)
-    _ORDER["graph"] = (units, pred, succ, eng, banks, ops)
-    fixed = TUNE.get("fixed", ORDER)
-    if fixed:
-        place = {u: j for j, u in enumerate(fixed)}
-        assert sorted(fixed) == list(range(len(units))) and all(place[p] < place[u] for u, ps in enumerate(pred) for p in ps)
-        _ORDER[key] = [n for u in fixed for n in units[u]]
-        return [ops[n] for n in _ORDER[key]]
-    level = [0.0] * len(units)
-    for u in range(len(units) - 1, -1, -1):
-        level[u] = hold[u] + late[u] + max([level[s] + 60.0 for s in succ[u]], default=0.0)
-    left = [len(p) for p in pred]
-    ready = [u for u in range(len(units)) if not left[u]]
-    done, free, bank, order = {}, {}, {}, []
-    moving = [0.0]
+    _ORDER["graph"] = (units, pred, None, eng, banks, hold, late, move, ops)
+    named = {}
+    for u, us in enumerate(units):
+        named.setdefault((eng[u],) + ops[us[0]]["tag"], []).append(u)
+    queue = {q: [u for t in range(RO + 1) for name in PLAN.get("%s%d" % (q, t), "").split()
+                 for u in named.get((q, name.rstrip("-"), t - name.count("-")), [])][::-1] for q in "VSPGYN"}
+    assert sorted(u for us in queue.values() for u in us) == list(range(len(units)))
+    hop = TUNE["hop"]
+    start, end, free, held, moving, order = {}, {}, {}, {}, 0.0, []
 
-    def start(u):
-        t = max([done[p] + (0.0 if eng[p] == eng[u] == "P" else 60.0) for p in pred[u]], default=0.0)
-        for b in banks[u]:
-            if b in bank and bank[b][0] != eng[u]:
-                t = max(t, bank[b][1] + 60.0)
-        return max(t, free.get(eng[u], 0.0))
+    def when(u):
+        t = max([start[p] if eng[p] == eng[u] == "P" else end[p] + hop for p in pred[u]] + [free.get(eng[u], 0.0)])
+        return max([t] + [x for b in banks[u] for q, x in held.get(b, {}).items() if q != eng[u]])
 
-    while ready:
-        est = {u: start(u) for u in ready}
-        first = min(ready, key=lambda u: (est[u], -level[u]))
-        u = max((v for v in ready if eng[v] == eng[first] and est[v] <= est[first] + TUNE["look"]),
-                key=lambda v: level[v] - TUNE["alpha"] * (est[v] - est[first]))
-        t = est[u]
-        done[u] = t + hold[u] + late[u]
-        if ops[units[u][0]].get("move"):
-            moving[0] = max(moving[0], t + 1500.0) + ops[units[u][0]]["move"]
-            done[u] = moving[0] + 500.0
-        if eng[u] is not None:
-            free[eng[u]] = t + hold[u]
+    while len(start) < len(units):
+        t, u = min((when(us[-1]), us[-1]) for us in queue.values() if us and all(p in start for p in pred[us[-1]]))
+        queue[eng[u]].pop()
+        start[u], free[eng[u]], end[u] = t, t + hold[u], t + hold[u] + late[u]
+        if move[u]:
+            moving = max(moving, t + 1300.0) + move[u]
+            end[u] = moving + 500.0
         for b in banks[u]:
-            bank[b] = (eng[u], done[u])
+            held.setdefault(b, {})[eng[u]] = end[u] + hop
         order += units[u]
-        ready.remove(u)
-        for s in succ[u]:
-            left[s] -= 1
-            if not left[s]:
-                ready.append(s)
     _ORDER[key] = order
     return [ops[n] for n in order]
 
@@ -142,10 +139,7 @@ def _arrange(ops):
 def _emit(g, T, ops):
     queues = {"V": g.vector, "S": g.scalar, "P": g.tensor, "G": g, "Y": g.sync}
     hist = {}
-    total = {}
-    for o in ops:
-        if o["grp"] is not None:
-            total[o["grp"]] = total.get(o["grp"], 0) + o["inc"]
+    total = {o["grp"]: o["inc"] for o in ops if o["grp"] is not None}
     known = {q: ({}, set()) for q in queues}
     after = {}
     gclock = {}
@@ -154,20 +148,20 @@ def _emit(g, T, ops):
         q = o["q"]
         deps = set()
         for (regs, wr) in ((o["r"], False), (o["w"], True)):
-            for (name, lo, hi) in regs:
-                for (m, lo2, hi2, wr2) in hist.get(name, []):
+            for x in regs:
+                for (m, y, wr2) in hist.get(x[0], []):
                     p = ops[m]
                     same = p["q"] == q and p["grp"] is None and o["grp"] is None
-                    if name == "ps" and not same:
-                        hit = lo // 512 <= (hi2 - 1) // 512 and lo2 // 512 <= (hi - 1) // 512
+                    if x[0] == "ps" and not same:
+                        hit = x[1] // 512 <= (y[2] - 1) // 512 and y[1] // 512 <= (x[2] - 1) // 512
                     else:
-                        hit = (wr or wr2) and lo < hi2 and lo2 < hi
-                    if hit and not (same and q == "P") and not (p["grp"] is not None and p["grp"] == o["grp"]):
+                        hit = (wr or wr2) and _meet(x, y)
+                    if hit and not (same and q == "P"):
                         deps.add(m)
         if o.get("final"):
             deps = set(m for m, p in enumerate(ops[:n]) if p["grp"] is not None and p["grp"] not in waited)
         o["waits"] = []
-        if q is not None:
+        if q != "N":
             ck, gs = known[q]
             for m in sorted(deps, reverse=True):
                 p = ops[m]
@@ -192,27 +186,22 @@ def _emit(g, T, ops):
                 c[q] = n
                 after[n] = (c, set(gs))
             else:
-                assert o["grp"] not in waited
-                c0, g0 = gclock.get(o["grp"], ({}, set()))
-                c = dict(c0)
-                for k, v in ck.items():
-                    c[k] = max(c.get(k, -1), v)
-                gclock[o["grp"]] = (c, set(g0) | set(gs))
+                gclock[o["grp"]] = (dict(ck), set(gs))
         else:
             gclock[o["grp"]] = ({}, set())
         for (regs, wr) in ((o["r"], False), (o["w"], True)):
-            for (name, lo, hi) in regs:
-                h = hist.setdefault(name, [])
-                if wr and name != "ps" and not o.get("part"):
-                    h[:] = [e for e in h if not (lo <= e[1] and e[2] <= hi)]
-                h.append((n, lo, hi, wr))
+            for x in regs:
+                h = hist.setdefault(x[0], [])
+                if wr and x[0] != "ps" and not o.get("part"):
+                    h[:] = [e for e in h if not (x[1] <= e[1][1] and e[1][2] <= x[2])]
+                h.append((n, x, wr))
     count = {}
     for o in ops:
         if o.get("sig"):
             count[o["q"]] = count.get(o["q"], 0) + 1
             o["cnt"] = count[o["q"]]
     for o in ops:
-        if o["q"] is None:
+        if o["q"] == "N":
             continue
         e = queues[o["q"]]
         best = {}
@@ -239,13 +228,17 @@ def rank_program(g, core, T, topo):
     if rank is None:
         return
     ops = []
+    now = ["load", 0]
+
+    def at(name, *k):
+        now[0] = name % k
 
     def a(name, lo=0, hi=None, st=1, p=None):
-        name = ALIAS.get(name, name)
         t = T[name]
         hi = t.shape[1] if hi is None else hi
         ap = t[slice(None) if p is None else p, slice(lo, hi) if st == 1 else slice(lo, hi, st)]
-        return (ap, [(name, lo, hi)], st != 1 or p is not None, len(range(lo, hi, st)), SCRATCH[name][2])
+        return (ap, [(name, lo, hi, st) + ((0, 128) if p is None else (p.start, p.stop))], st != 1 or p is not None,
+                len(range(lo, hi, st)), SCRATCH[name][2])
 
     def ind(win, off):
         return (win[0].indirect(off[0]), win[1] + off[1], False, 0, win[4])
@@ -265,21 +258,21 @@ def rank_program(g, core, T, topo):
 
     def op(q, fn, outs, ins, grp=None, inc=16, dma=True, rate=None, **more):
         o = {"q": q, "fn": fn, "w": regs(*outs), "r": regs(*ins), "grp": grp, "inc": inc, "dma": dma,
-             "part": any(x[2] for x in outs), "hold": 0.0, "late": 0.0}
+             "part": any(x[2] for x in outs), "hold": 0.0, "late": 0.0, "tag": tuple(now)}
         big = [x for x in ins if isinstance(x, tuple) and x[3] != 1]
         if grp is not None:
-            o["hold"], o["late"] = (100.0, 2500.0) if dma else (500.0 if q else 0.0, 3000.0 if q else 500.0)
+            o["hold"], o["late"] = (60.0, 2500.0) if dma else ((500.0, 3000.0) if q == "G" else (0.0, 500.0))
         elif q == "P":
-            o["hold"], o["late"] = 10 + 0.52 * max(64, outs[0][3]) * (4 if ins[0][4] == F32 else 1), 140.0
+            o["hold"], o["late"] = 5 + 0.44 * max(64, outs[0][3]) * (4 if ins[0][4] == F32 else 1), 50.0
         elif q == "G":
-            o["hold"] = 130 + 2.08 * outs[0][3]
+            o["hold"], o["late"] = 150 + 1.66 * outs[0][3], 400.0
+        elif any(x[3] == 0 for x in big):
+            o["gn"] = outs[0][3]
+            o["hold"] = 60 + 0.83 * TUNE["gather"] * outs[0][3]
         else:
-            o["gn"] = outs[0][3] if any(x[3] == 0 for x in big) else 0
-            if o["gn"]:
-                rate = TUNE["gather"]
-            elif rate is None:
-                rate = 0.5 if q == "V" and all(x[4] in (BF, U16) for x in big + [outs[0]]) else 1.0
-            o["hold"] = 55 + 1.04 * max(64, rate * outs[0][3])
+            if rate is None:
+                rate = 0.5 if q == "V" and all(x[4] in (BF, U16, F16) for x in big + [outs[0]]) else 1.0
+            o["hold"] = (30 if q == "V" else 105) + 0.83 * max(64, rate * outs[0][3])
         o.update(more)
         ops.append(o)
 
@@ -299,8 +292,8 @@ def rank_program(g, core, T, topo):
     def ms(out, c):
         op("V", lambda e: e.memset(out[0], c), [out], [])
 
-    def scan(out, d0, d1, o0, o1):
-        op("V", lambda e: e.tensor_tensor_scan(out[0], d0[0], d1[0], 0.0, o0, o1), [out], [d0, d1])
+    def scan(out, d0, d1, o0, o1, first=0.0):
+        op("V", lambda e: e.tensor_tensor_scan(out[0], d0[0], d1[0], first, o0, o1), [out], [d0, d1])
 
     def act(out, x, f=AF.Identity, bias=0.0, scale=1.0, acc=None):
         if acc is None:
@@ -308,12 +301,15 @@ def rank_program(g, core, T, topo):
         else:
             op("S", lambda e: e.activation(out[0], x[0], f, bias=val(bias), scale=val(scale), accum_out=acc[0]), [out, acc], [x, bias, scale])
 
-    def mm(out, l, r, start, stop, **more):
+    def gcp(out, x):
+        op("G", lambda e: e.affine_select(out[0], x[0], [[0, out[3]]], OP.is_ge, 0.0, 0, 0), [out], [x])
+
+    def mm(out, l, r, start=True, stop=True, **more):
         op("P", lambda e: e.matmul(out[0], l[0], r[0], start, stop), [out], [l, r], **more)
 
-    def mmg(items):
-        for j, (out, l, r) in enumerate(items):
-            mm(out, l, r, j == 0, j == len(items) - 1, join=j > 0)
+    def mms(out, items):
+        for j, x in enumerate(items):
+            mm(*((out,) + x)[-3:], j == 0, j == len(items) - 1, join=j > 0)
 
     def iota(out, pat, base=0, cm=0, small=True):
         if small:
@@ -352,389 +348,501 @@ def rank_program(g, core, T, topo):
         for d in range(N - 1):
             r = (rank - sign * (1 + d)) % N
             got += len(masks(T.cores[r], [T.cores[(r + sign * (1 + k)) % N] for k in range(N - 1)])[d])
-        op(None, None, dsts, [], "arr%d" % tag, got, False)
+        op("N", None, dsts, [], "arr%d" % tag, got, False)
 
-    R0, R1, R8 = slice(0, 128, 16), slice(1, 128, 16), slice(0, 8)
+    P0, P8, P33, P97 = slice(0, 1), slice(0, 8), slice(0, 33), slice(0, 97)
+    part = lambda r: slice(r, r + 1)
     col = lambda j: a("col", j, j + 1)
     mat = lambda j: a("mats", 128 * j, 128 * (j + 1))
-    sel = lambda name, j: a(name, 128 * j, 128 * (j + 1))
-    NEG, B2, BN, EP, EN, HALF = range(6)
-    PM, PG, PP, H0, H1, SC0, SC1, BA0, BA1, BB0, BB1, FS0, FS1, FB0, FB1, L01 = range(16)
-    CD, CF, CQ, CG, CI = 0, 512, 640, 896, 1024
-    one = a("lc", p=slice(0, 1))
-    row = lambda lo, n: a("cv", lo, lo + n, p=slice(0, 1))
+    sel = lambda name, j, **kw: a(name, 128 * j, 128 * (j + 1), **kw)
+    MATS = [-1.0, 2048.0, BIG, 64.0 * S, 0.25, 0.75, 8.25, float(S), -2048.0]
+    NEG, T2K, PB, FLAG, Q1, Q3, E8, K4K, N2K = range(len(MATS))
+    PP, PM, PG, H0, H1, SC0, SC1, BB0, BB1, BK0, BK1, FS0, FS1, FB0, FB1 = range(15)
+    CD, CO, CB, CQ = 0, 512, 1024, 1280
+    one, ones = a("lc", 0, 128, p=P0), a("lc", 0, 128, p=P97)
+    eye, blk = a("eye"), a("blk")
     xt = lambda t, *k: a("xt%d" % (t % 2), *k)
     wn = lambda t, *k: a("wn%d" % (t % 2), *k)
-    ot = lambda t, *k, **kw: a("ot%d" % (t % 2), *k, **kw)
-    half = lambda name, t, lo=0, hi=256: a(name, 256 * (t % 2) + lo, 256 * (t % 2) + hi)
-    slot = lambda name, t, lo=0, hi=256: a(name, 256 * t + lo, 256 * t + hi)
-    lanes = lambda name, m: a(name, m, NV, ST)
+    slot = lambda name, t, lo=0, hi=256, **kw: a(name, 256 * t + lo, 256 * t + hi, **kw)
+    lanes = lambda name, m, lo=0, hi=256, **kw: a(name, m + ST * lo, ST * hi, ST, **kw)
     ch = lambda name, c: a(name, 1024 * c, 1024 * (c + 1))
-    pair = [0]
+    ps = lambda lo, n, **kw: a("ps", lo, lo + n, **kw)
     pair_of = {}
-    pp = lambda key: a("ps", pair_of[key], pair_of[key] + 1024)
-    PD, XV, P2, P3 = a("ps", 3072, 3328), a("ps", 3328, 3584), a("ps", 3584, 3840), a("ps", 3840, 4096)
-    PA, PGO = a("ps", 3900, 3901), a("ps", 3840, 3888)
+    x, y, z = 0, 1024, 2048
+    for t in range(RO):
+        if t >= 3:
+            pair_of["q", t] = x
+            x, y, z = y, z, x
+        for key, lo in ((("a", 0), x), (("a", 1), y), (("a", 2), z), (("a", 3), x), (("b", 0), y), (("b", 1), z), (("b", 2), x),
+                        (("o", 0), y), (("b", 3), z), (("o", 1), x)):
+            pair_of[key[0], t, key[1]] = lo
+        pair_of["s", t] = z
+        x, y = y, x
+    take = lambda key: pair_of[key]
+
+    pp = lambda key: ps(pair_of[key], 1024)
+    B0, B1, C1 = ps(3072, 256), ps(3328, 256), ps(3840, 256)
+    PA, PGO = ps(3072, 1), ps(3840, 48)
+    KEY, TURN = (3584, 3200), (3712, 3072)
     yv = a("s3", 15, 4096, 16)
 
+    def diagonal(lo, name, h):
+        for k in range(16):
+            mm(a("ps", lo + k, lo + 128, 16), a(name, 2048 * h + k, 2048 * (h + 1), 16), a("eye", k, 128, 16), join=k % 8 > 0)
+
     dma("Y", "lf", a("fst"), hbm(T.f0[:]))
-    for j in range(4):
-        dma("Y", "lk%d" % j, a("ktb", 768 * j, 768 * (j + 1)), hbm(T.kt[:, 768 * j:768 * (j + 1)]), 390)
+    for j in range(len(CUTS) - 1):
+        lo, hi = 192 * CUTS[j], 192 * CUTS[j + 1]
+        dma("Y", "lk%d" % j, a("ktb", lo, hi), hbm(T.kt[:, lo:hi]), (hi - lo) // 2)
     dma("Y", "lxg", a("xt0", NV, NW), hbm(T.x0[:, NV:NW]), 200)
     dma("Y", "lt", a("thi"), hbm(T.th[:]))
     dma("Y", "ls", a("shi"), hbm(T.shw[:]))
     dma("Y", "lx0", a("xt0", 0, NV), hbm(T.x0[:, 0:NV]), 790)
     dma("Y", "lx1", a("xt1", 0, NV), hbm(T.x0[:, 0:NV]), 790)
 
+    def put(out, c):
+        if now[0] in TUNE["cv"]:
+            ms(out, c)
+        else:
+            act(out, out, bias=c, scale=0.0)
+
+    def times(out, x, c):
+        if now[0] in TUNE["cv"]:
+            ts(out, x, c, OP.mult)
+        else:
+            act(out, x, scale=c)
+
+    at("c0")
     iota(a("pi", 0, 1), [[0, 1]], 0, 1, False)
     iota(a("qg"), [[1, 8], [0, 16]])
     iota(a("q128"), [[1, 128]])
-    iota(a("cv", CI, CI + 256), [[1, 256]])
-    iota(a("bas"), [[16, 48]], 256)
+    iota(a("rev"), [[-1, 8]], 15)
+    iota(a("gt", NV, NW), [[0, NW - NV]], -64 * S)
     ts(a("pi", 1, 2), a("pi", 0, 1), 15, OP.bitwise_and)
     ts(a("pi", 2, 3), a("pi", 0, 1), 4, OP.arith_shift_right)
-    ms(a("gt", NV, NW), 16.0 * S)
-    cp(col(PM), a("pi", 1, 2))
-    cp(col(PG), a("pi", 2, 3))
-    cp(col(PP), a("pi", 0, 1))
+    cp(a("col", PP, PG + 1), a("pi", 0, 3))
+    ts(blk, a("qg"), col(PG), OP.is_equal)
+    ts(a("m16"), a("q128", 0, 17), col(PM), OP.is_equal)
     ts(col(H0), col(PM), 7.5, OP.is_lt)
     ts(col(H1), col(PM), 7.5, OP.is_gt)
-    ts(a("blk"), a("qg"), col(PG), OP.is_equal)
-    ts(a("m16"), a("q128", 0, 16), col(PM), OP.is_equal)
-    ts(a("col", FS0, FS1 + 1), a("col", H0, H1 + 1), 64.0, OP.mult)
-    ts(a("col", FB0, FB1 + 1), a("col", H0, H1 + 1), 16.0, OP.mult)
     tt(a("m8"), a("m16", 0, 8), a("m16", 8, 16), OP.add)
-    ts(a("col", SC0, SC1 + 1), a("col", H0, H1 + 1), 1.0 / S, OP.mult)
-    ts(a("col", BA0, BA1 + 1), a("col", H0, H1 + 1), 239.0625, OP.mult, 0.46875, OP.add)
-    ts(a("col", BB0, BB1 + 1), a("col", H0, H1 + 1), 479.53125, OP.mult, -240.0, OP.add)
+    ts(a("bks"), blk, float(S), OP.mult)
+    ts(eye, a("q128"), col(PP), OP.is_equal)
+    hh2 = a("col", H0, H1 + 1)
+    ts(a("col", FS0, FS1 + 1), hh2, 128.0, OP.mult)
+    ts(a("col", FB0, FB1 + 1), hh2, -64.0, OP.mult)
+    ts(a("col", SC0, SC1 + 1), hh2, 1.0 / S, OP.mult)
+    ts(a("col", BK0, BK1 + 1), hh2, 159.0625, OP.mult, 0.46875, OP.add)
     for j in range(8):
-        ts(sel("sw2", j), a("blk"), a("m8", j, j + 1), OP.mult, float(S), OP.mult)
+        times(sel("sw2", j), a("bks"), a("m8", j, j + 1))
     for h in range(2):
         ts(a("f2", 192 * h, 192 * (h + 1)), a("fst"), col(FS0 + h), OP.mult, col(FB0 + h), OP.add)
     for j in range(8):
-        mm(a("ps", 512 * j, 512 * j + 384), sel("sw2", j), a("f2"), True, True)
-    ts(a("eye"), a("q128"), col(PP), OP.is_equal)
-    ms(a("lc", p=slice(0, 64)), 0.0)
-    ms(a("cv", CD, CD + 512, p=slice(0, 32)), 0.0)
-    ms(a("cv", CD, CD + 512, p=slice(32, 64)), 1.0 / 32)
-    ms(a("cv", CF, CF + 128), -768.0 * S * 512)
-    ts(mat(NEG), a("eye"), -1.0, OP.mult)
-    ms(a("lc", p=slice(0, 1)), 1.0)
-    ms(a("lc", p=slice(32, 33)), 1.0)
-    ms(a("cv", CD + 15, CD + 512, 16, p=slice(0, 32)), -80.0 * S)
-    ms(a("cv", CD + 15, CD + 512, 16, p=slice(32, 64)), -15.0 / 32)
-    ts(a("col", 16, 32), a("m16"), -2048.0, OP.mult)
-    for k in range(16):
-        act(sel("dga", k), a("eye"), scale=col(16 + k))
-    ts(col(L01), col(PM), 1.5, OP.is_lt)
-    iota(a("slo"), [[0, 2048]])
-    ts(a("b01"), a("blk"), col(L01), OP.mult)
+        mm(ps(512 * j, 384), sel("sw2", j), a("f2"))
+    at("c1")
+    ts(a("col", BB0, BB1 + 1), hh2, 512.0, OP.mult, -240.0, OP.add)
+    ts(a("c8", 0, 8), a("m16", 0, 8), -float(S), OP.mult)
+    ts(a("rev"), a("rev"), col(PM), OP.is_equal)
+    tt(a("md"), a("m16", 1, 17), a("m16", 0, 16), OP.subtract)
+    ts(a("thm"), a("qg"), col(PP), OP.is_equal, -1.0, OP.mult)
+    tt(a("c8", 8, 16), a("c8", 0, 8), a("rev"), OP.subtract)
+    iota(a("lc"), [[0, 384]])
+    iota(a("cv", CD, CO), [[0, CO - CD]])
+    for lo, scales in ((0, (1, 1, S, S * S // 2)), (128, (1, 1, 1, S // 2)), (256, (-1, -1))):
+        at("c14" if lo == 0 else "c8")
+        for r, c in enumerate(scales):
+            put(a("lc", lo, lo + 128, p=part(32 * r)), float(c))
+    at("c14")
+    times(mat(NEG), eye, MATS[NEG])
+    put(a("cv", CD, CO, p=part(32)), 1.0 / 32)
+    for r, c in ((0, -1920.0), (32, -0.5), (64, -32.0)):
+        put(a("cv", CD + 15, CO, 16, p=part(r)), c)
+    at("c2")
+    times(a("sw3"), a("sw2"), 17.0 / S)
+    at("c3")
     for j in range(8):
-        act(sel("sw3", j), sel("sw2", j), scale=17.0 / S)
-    for k in range(16):
-        act(a("slo", 128 * k + k, 128 * (k + 1), 16), a("b01", k, 128, 16))
-    act(a("dgb"), a("dga"), scale=-128.0)
-    for j, src, c in ((B2, "blk", 2.0), (BN, "blk", -1.0), (EP, "eye", 2.0 ** -18), (EN, "eye", -2.0 ** -18), (HALF, "eye", 0.5)):
-        act(mat(j), a(src), scale=c)
-    iota(a("va"), [[192, 16], [0, 16]])
-    iota(a("vb"), [[1, 3], [0, 16], [12, 16]])
+        times(sel("csel", j), blk, a("c8", 8 + j, 9 + j))
+    at("c4")
+    for j in range(1, len(MATS)):
+        times(mat(j), eye, MATS[j])
+    times(a("b17"), blk, 17.0)
+    at("c5")
+    times(a("r8", 0, 8), a("blk", 0, 128, 16), a("m16", 0, 1))
+    times(a("r8", 16, 24), a("eye", 0, 8), -2.0)
+    times(a("r8", 8, 16), a("r8", 0, 8), -1.0)
+    for k in range(17):
+        at(("c6", "c12", "c13")[k // 6])
+        times(sel("dgd", k), mat(T2K), a("md", k, k + 1) if k < 16 else a("m16", 0, 1))
+    at("g1")
+    gcp(a("ffl"), a("fst"))
+    gcp(a("fb"), a("fst"))
+    gcp(a("shu"), a("shi"))
+    iota(a("bas"), [[16, 48]], 256)
+    at("x")
     exchange(RO, 1, [a("xt0", NV + 256 * d, NV + 256 * (d + 1)) for d in range(3)],
              [a("wn0", 256 * (d + 1), 256 * (d + 2)) for d in range(3)])
-    iota(a("vt"), [[1, 2], [12, 256]])
+    at("g2")
+    iota(a("rs3"), [[0, 1024]], 1)
+    iota(a("rs3", 0, 1024, 16), [[0, 64]])
+    at("g3")
+    iota(a("cv", CO, CB), [[0, 64], [4, 8]], -30)
+    at("g4")
+    iota(a("cv", CB, CQ + 256), [[0, CQ + 256 - CB]], -34)
+    at("c9")
+    for r, c in ((0, -1920.0), (32, 0.0), (64, -1920.0)):
+        put(a("cv", CO, CB, p=part(r)), c)
+    at("c10")
+    for r, c in ((0, 0.0), (32, 0.0), (64, -128.0)):
+        put(a("cv", CB, CQ, p=part(r)), c)
+    at("g5")
+    iota(a("rs2"), [[0, 1024]], -1)
+    iota(a("rs2", 0, 1024, 8), [[0, 128]])
+    at("g6")
+    iota(a("vv"), [[1, 3], [0, 16], [12, 16]])
+    at("g7")
+    iota(a("vv", p=P0), [[0, 3], [192, 16], [0, 16]], -1920)
+    at("c11")
+    put(a("vv", p=part(64)), 1920.0)
+    put(a("vv", p=part(96)), -34.0)
+    at("g8")
+    iota(a("cap"), [[0, 256]], 64)
+    iota(a("cnm"), [[0, 128]], 1)
+    iota(a("cnt"), [[0, 4]])
+    at("c7")
+    put(a("cnt", 0, 1, p=part(32)), 2039.5)
+    ts(a("thc"), a("thi"), -2040.0, OP.add)
+    ts(a("bs16"), a("bas"), col(PM), OP.add)
+    put(a("cv", CQ, CQ + 256, p=P0), -0.25)
+    dma("Y", "dff", a("ff", p=P8), a("ffl"))
+    dma("Y", "df8", a("f8", p=P8), a("fb"), 30)
+    dma("Y", "dth", a("thf", p=P8), a("thc"), 30)
 
-    def late_constants():
-        ms(a("cv", CQ, CQ + 256), -0.25)
-        ms(a("cv", CG, CG + 48), 130048.0)
-        iota(a("rs3"), [[0, 1024]], 1)
-        iota(a("rs5"), [[0, 768]], 1)
-        ms(a("rs3", 0, 1024, 16), 0.0)
-        ms(a("rs5", 0, 768, 256), 0.0)
-        for name in ("ot0", "ot1"):
-            for lo in range(0, 4352, 1088):
-                iota(a(name, lo, lo + 1088), [[0, 1088]])
-        ts(a("thm"), a("qg"), col(PP), OP.is_equal, -1.0, OP.mult)
-        ts(a("cnm"), a("q128"), 0.0, OP.mult, a("m16", 0, 1), OP.add)
-        ts(a("bas"), a("bas"), col(PM), OP.add)
-        cp(a("ffl"), a("fst"))
-        dma("Y", "dff", a("ff", p=R0), a("ffl"))
-        dma("Y", "dva", a("ot0", 0, 256, p=R0), a("va", p=R0))
-        dma("Y", "dva", a("ot1", 0, 256, p=R0), a("va", p=R0))
-        cp(a("thc"), a("thi"))
-        dma("Y", "dth", a("thf", p=R8), a("thc"), 30)
-        cp(a("shu"), a("shi"))
-
-    def entries(t, src, off):
-        ts(a("ci"), src, S - 1, OP.bitwise_and)
-        ts(half("own", t), src, 1.0 / 32 - off, OP.add)
-        cp(half("c16", t), a("ci"))
+    def entries(t, src, lo, hi):
+        name = lambda x: at(x) if t >= 3 else at("e%d%d", t, lo // 128)
+        name("ci")
+        cast = gcp if t in TUNE["eg"] else cp
+        ts(slot("ci", t % 3, lo, hi), src, S - 1, OP.bitwise_and)
+        if t < 3:
+            cast(slot("kf", t, lo, hi), src)
+        name("c16")
+        cast(slot("c16", t, lo, hi), slot("ci", t % 3, lo, hi))
+        if t in (1, 2):
+            name = lambda x: at("f%d%d", t, lo // 128)
+        name("cf")
+        ts(slot("cf", t, lo, hi), slot("c16", t, lo, hi), -1920.0, OP.add)
+        name("wa")
         for h in range(2):
-            act(a("w2a", 512 * (t % 2) + h, 512 * (t % 2 + 1), 2), half("own", t), bias=col(BA0 + h), scale=col(SC0 + h))
+            act(a("w2a", 512 * t + 2 * lo + h, 512 * t + 2 * hi, 2), slot("kf", t, lo, hi), bias=col(BK0 + h), scale=col(SC0 + h))
 
-    def gat_f(t, c, on_vector=False):
-        (cp if on_vector else act)(ch("fg", c), ind(a("gt"), half("o16", t - 3, 64 * c, 64 * (c + 1))))
+    def gather(name, key, t, c, win, off):
+        at({"fv": "F%d", "gv": "G%d", "xv": "X%d"}[key], c)
+        (cp if c in TUNE[key].get(t, ()) else act)(ch(name, c), ind(win, off))
 
     def give_back(t):
-        lo = 1024 * ((pair[0] + 2) % 3) + 512
-        PF, PT = a("ps", lo, lo + 256), a("ps", lo + 256, lo + 512)
+        u = t - 3
         for c in range(4):
-            mmg([(a("ps", lo + 64 * c, lo + 64 * (c + 1)), sel("dga", k), a("fg", 1024 * c + k, 1024 * (c + 1), 16)) for k in range(16)])
-        ts(PF, PF, -900000.0 * 512, OP.is_gt, -1.0, OP.mult)
-        tt(PT, half("dkm", t - 3), PF, OP.mult)
-        tt(lanes("gt", t % 3), lanes("gt", t % 3), PT, OP.add)
-        tt(a("kin"), slot("kp", t - 3), PT, OP.add)
-        act(half("frn", t - 3), PF)
-        entries(t, a("kin"), 16.0 * S)
+            gather("xg", "fv", t, c, a("gt"), slot("o16", u, 64 * c, 64 * (c + 1)))
+        lo = take(("q", t))
+        Q, T2, PF = ps(lo, 256), ps(lo + 512, 256), ps(lo + 768, 256)
+        at("pq")
+        mm(PF, mat(FLAG), slot("fs", u))
+        for h in range(2):
+            at("Q%d", h)
+            diagonal(lo + 256 + 128 * h, "xg", h)
+            at("q%d", h)
+            ts(sel("zt", h), ps(lo + 256 + 128 * h, 128), 0.0, OP.is_ge, 0.5, OP.subtract)
+            at("H%d", h)
+            mms(ps(lo + 128 * h, 128), [(mat(FLAG), slot("ne", u, 128 * h, 128 * (h + 1))), (sel("zt", h), mat(FLAG))])
+        at("t1")
+        tt(a("t1"), slot("kp", u), Q, OP.min)
+        at("t2")
+        tt(T2, slot("kf", u), Q, OP.subtract)
+        at("rs")
+        act(slot("rs", u), Q, AF.Sign, bias=-1.0)
+        at("kin")
+        tt(a("kin"), a("t1"), T2, OP.max)
+        at("gb")
+        tt(lanes("gt", t % 3), a("kin"), PF, OP.min)
+        at("kf")
+        tt(slot("kf", t), a("t1"), T2, OP.max)
+        entries(t, a("kin"), 0, 256)
 
     def weights(key, name, rhs, base, c):
-        pair_of[key] = 1024 * (pair[0] % 3)
-        pair[0] += 1
+        at("W%d" if key[0] == "a" else "V%d", c)
+        take(key)
         for b in range(2):
             lo = pair_of[key] + 512 * b
             for j in range(8):
-                mm(a("ps", lo + j, lo + 512, 8), sel(name, j), a(rhs, base + 128 * c + 64 * b, base + 128 * c + 64 * (b + 1)),
-                   True, True, join=j > 0)
+                mm(a("ps", lo + j, lo + 512, 8), sel(name, j), a(rhs, base + 128 * c + 64 * b, base + 128 * c + 64 * (b + 1)), join=j > 0)
 
-    w2 = lambda t, c: weights(("a", t, c), "sw2", "w2a", 512 * (t % 2), c)
+    w2 = lambda t, c: weights(("a", t, c), "sw2", "w2a", 512 * t, c)
     w3 = lambda t, c: weights(("b", t, c), "sw3", "w2b", 0, c)
-
-    def gat_g(t, c):
-        (cp if (TUNE["gv"] >> t) & 1 and c == 1 else act)(ch("gg", c), ind(a("gt"), half("c16", t, 64 * c, 64 * (c + 1))))
+    gat_g = lambda t, c: gather("gg", "gv", t, c, a("gt"), slot("c16", t, 64 * c, 64 * (c + 1)))
+    gat_x = lambda t, c: gather("xg", "xv", t, c, xt(t), a("d16", 64 * c, 64 * (c + 1)))
 
     def zr(t, c):
-        tt(ch("zz", c), ch("gg", c), pp(("a", t, c)), OP.subtract)
-        if (TUNE["rs"] >> (4 * t + c)) & 1:
-            act(ch("rr", c), ch("zz", c), AF.Relu, bias=160.0 * S)
+        at("Z%d", c)
+        tt(ch("zz", c), pp(("a", t, c)), ch("gg", c), OP.subtract)
+        at("R%d", c)
+        if c in TUNE["rs"].get(t, ()):
+            act(ch("rr", c), ch("zz", c), AF.Relu, bias=160.0 * S, scale=-1.0)
+            here, nxt = mat(NEG), eye
         else:
-            ts(ch("rr", c), ch("zz", c), -160.0 * S, OP.max, 160.0 * S, OP.add)
+            ts(ch("rr", c), ch("zz", c), 160.0 * S, OP.min, 160.0 * S, OP.subtract)
+            here, nxt = eye, mat(NEG)
+        at("A%d", c)
+        for b in range(2):
+            mm(ps(pair_of[("a", t, c)] + 512 * b, 512), ones, a("cv", CD, CO, p=P97), True, False)
+        at("D%d", c)
         for b in range(2):
             lo, x = pair_of[("a", t, c)] + 512 * b, 1024 * c + 512 * b
-            mmg([(a("ps", lo, lo + 512), a("lc", p=slice(0, 33)), a("cv", CD, CD + 512, p=slice(0, 33))),
-                 (a("ps", lo, lo + 512), mat(NEG), a("rr", x, x + 512)),
-                 (a("ps", lo, lo + 511), a("eye"), a("rr", x + 1, x + 512)),
-                 (a("ps", lo + 15, lo + 511, 16), mat(NEG), a("rr", x + 16, x + 512, 16))])
+            mm(ps(lo, 512), here, a("rr", x, x + 512), False, False)
+            mm(ps(lo, 511), nxt, a("rr", x + 1, x + 512), False, False)
+            mm(a("ps", lo + 15, lo + 511, 16), here, a("rr", x + 16, x + 512, 16), False, True, join=True)
 
     def scan2(t, c):
-        scan(ch("so", c), ch("gg", c), pp(("a", t, c)), OP.max, OP.add)
-
-    def flag(h):
-        out = a("ps", 3072 + 128 * h, 3072 + 128 * (h + 1))
-        mmg([(out, one, row(CF, 128))] + [(out, sel("dga", k), a("zz", 2048 * h + k, 2048 * (h + 1), 16)) for k in range(16)])
+        at("S%d", c)
+        scan(ch("so", c), ch("gg", c), pp(("a", t, c)), OP.max, OP.add, -40.0 * S)
 
     def own_key(t, h):
-        tt(a("ps", 3328 + 128 * h, 3328 + 128 * (h + 1)), half("own", t, 128 * h, 128 * (h + 1)),
-           a("ps", 3072 + 128 * h, 3072 + 128 * (h + 1)), OP.min)
+        at("K%d", h)
+        diagonal(TURN[h], "zz", h)
+        at("zt%d", h)
+        act(sel("zt", h), ps(TURN[h], 128), bias=-256.0 * S)
+        at("J%d", h)
+        mms(ps(KEY[h], 128), [(eye, slot("cf", t, 128 * h, 128 * (h + 1))), (sel("zt", h), eye)])
 
     def winners(t, h):
         lo, hi = 128 * h, 128 * (h + 1)
-        b = a("ps", 3584 + lo, 3584 + hi)
-        tt(b, a("so", 2048 * h + 15, 2048 * (h + 1), 16), a("ps", 3328 + lo, 3328 + hi), OP.max)
-        ts(slot("kp", t, lo, hi), b, 16.0 * S, OP.add)
+        b = ps(KEY[h], 128)
+        at("b%d", h)
+        tt(b, a("so", 2048 * h + 15, 2048 * (h + 1), 16), b, OP.max)
+        at("kp%d", h)
+        ts(slot("kp", t, lo, hi), b, 32.0 * S + 1920.25, OP.add)
+        at("cj%d", h)
+        ts(a("cj", lo, hi), slot("kp", t, lo, hi), S - 1, OP.bitwise_and)
+        at("d%d", h)
+        (gcp if h in TUNE["dg"] else cp)(a("d16", lo, hi), a("cj", lo, hi))
+        at("fr%d", h)
         tt(a("fra", lo, hi), b, slot("kp", t, lo, hi), OP.subtract)
-        if t < 2:
-            tt(half("dkn", t, lo, hi), b, a("ktb", t + ST * lo, ST * hi, ST), OP.subtract)
+        at("wb%d", h)
         for j in range(2):
             act(a("w2b", 2 * lo + j, 2 * hi, 2), b, bias=col(BB0 + j), scale=col(SC0 + j))
-        ts(a("cj", lo, hi), slot("kp", t, lo, hi), S - 1, OP.bitwise_and)
-        cp(a("d16", lo, hi), a("cj", lo, hi))
-
-    def gat_x(t, c):
-        act(ch("xg", c), ind(xt(t), a("d16", 64 * c, 64 * (c + 1))))
+        at("uu%d", h)
+        act(a("uu", lo, hi), a("fra", lo, hi), AF.Abs, bias=2.0 ** 23 + 64 * 1920.5 - 15, scale=64.0)
 
     def min3(t, c):
+        at("M%d", c)
         tt(ch("t3", c), ch("xg", c), pp(("b", t, c)), OP.min)
 
-    def scan3(c):
+    def scan3(t, c):
+        at("T%d", c)
         scan(ch("s3", c), a("rs3"), ch("t3", c), OP.mult, OP.max)
+
+    def pick(t, h):
+        base = take(("o", t, h))
+        for b in range(2):
+            at("P%d", 2 * h + b)
+            lo, x = base + 512 * b, 128 * h + 64 * b
+            mm(ps(lo, 512), ones, a("cv", CO, CO + 512, p=P97), True, False)
+            for j in range(16):
+                l, r = (mat(PB), a("uu", x, x + 64)) if j < 8 else (sel("csel", j - 8), slot("cf", t, x, x + 64))
+                mm(a("ps", lo + j % 8, lo + 512, 8), l, r, False, j == 15, join=j % 8 > 0)
+        at("U%d", h)
+        scan(ch("so2", h), a("rs2"), ps(base, 1024), OP.mult, OP.min)
+
+    def unpack(t):
+        lo = pair_of[("s", t)]
+        SC, K1, K2 = ps(lo + 512, 256), ps(lo + 768, 256), ps(lo + 256, 256)
+        own = (a("lc", 128, 256, p=P97), slot("vv", t % 3, p=P97))
+        at("sc")
+        ts(SC, a("fra"), 15.0 / 64 - 32 * S - 1920.5, OP.is_lt, 1.0 / S, OP.max)
+        at("k1")
+        mms(K1, [own, (mat(K4K), a("uu"))] + ([(mat(N2K), slot("rs", t - 3)), (mat(N2K), a("rs3", 1, 1024, 4))] if t >= 3 else []))
+        if t >= 3:
+            at("k2")
+            mms(K2, [(own[0], a("cv", CB, CQ, p=P97)), (mat(K4K), a("uu")), (mat(T2K), slot("rs", t - 3)), (eye, slot("of", t - 3))])
+        at("xa")
+        act(a("xa"), a("so2", 7, 2048, 8), AF.Abs)
+        at("x1")
+        tt(a("x1"), a("xa"), SC, OP.mult)
+        at("x2")
+        tt(a("x1"), a("x1"), K1, OP.max)
+        if t >= 3:
+            at("x3")
+            tt(a("x1"), a("x1"), K2, OP.max)
+        at("x4")
+        ts(a("x3"), a("x1"), 2.0, OP.mult, -0.4375, OP.add)
+        at("og")
+        ts(slot("og", t), a("x3"), 1, OP.arith_shift_right, S - 1, OP.bitwise_and)
+        at("yo")
+        if t == 3:
+            tt(a("yoa"), slot("og", 2), slot("og", 3), OP.add)
+        if t == 4:
+            tt(a("yob"), a("yoa"), slot("og", 4), OP.add)
+            dma("Y", "oyo", hbm(T.yo[:]), a("yob"))
+
+    def keep_origins(t):
+        at("o16")
+        gcp(slot("o16", t), slot("og", t))
+        at("of")
+        ts(slot("of", t), slot("o16", t), -1920.0, OP.add)
+        at("pv")
+        mms(C1, [(eye, slot("of", t)), (a("lc", 256, 384, p=P33), slot("vv", t, p=P33))])
+        at("ne")
+        ts(slot("ne", t), C1, 0.0, OP.is_equal, 0.5, OP.add)
 
     def status(t):
         m = t % 3
-        xv = xt(t, m, NV, ST)
-        mm(XV, a("eye"), xv, True, True)
-        mm(PD, a("thm", p=R8), a("thf", 256 * m, 256 * (m + 1), p=R8), True, False, lock=[("ps", 3072, 3584)])
-        mm(PD, mat(BN), xv, False, False, join=True)
-        tt(a("mxv"), yv, XV, OP.max)
-        mm(PD, mat(BN), yv, False, False, lock=[("ps", 3072, 3584)])
-        mm(PD, mat(B2), a("mxv"), False, True, join=True)
-        mmg([(P2, mat(EN), xv), (P2, mat(EP), yv)])
-        act(a("yc"), yv)
-        last = t == RO - 1
-        ts(slot("fd", t) if last else PD, PD, 0.0 if t == 0 else a("am", 0, 1), OP.is_lt, 64.0 * S, OP.mult)
-        if not last:
-            tt(lanes("gt", m), slot("kp", t), PD, OP.add)
-            act(slot("fd", t), PD)
+        PD = ps(take(("s", t)), 256)
+        at("pd")
+        mms(PD, [(mat(NEG), xt(t, m, NV, ST)), (eye, yv)])
+        at("ad")
+        act(a("ad"), PD, AF.Abs)
+        at("pb")
+        mms(B0, [(a("thm", p=P8), slot("thf", m, p=P8)), (blk, a("ad"))])
+        at("fs")
+        act(slot("fs", t), B0, AF.Sign, bias=2039.5 if t == 0 else a("am", 0, 1), scale=-1.0)
+        if t < RO - 1:
+            at("pf")
+            mm(C1, mat(FLAG), slot("fs", t))
+            at("gt")
+            tt(lanes("gt", m), slot("kp", t), C1, OP.min)
 
     def new_x(t):
         m = t % 3
-        xv = xt(t, m, NV, ST)
-        tt(a("tt4"), slot("fd", t), P2, OP.mult)
-        mmg([(P3, one, row(CQ, 256)), (P3, mat(HALF), xv), (P3, mat(HALF), a("yc")), (P3, mat(HALF), a("tt4"))])
-        ts(wn(t, 0, 256), P3, 1.5 * 2 ** 23, OP.add, -1.5 * 2 ** 23, OP.add)
-        tt(a("ne"), wn(t, 0, 256), XV, OP.not_equal)
-        mm(P2, a("blk"), a("ne"), True, True)
-        cp(xt(t + 1, m, NV, ST), wn(t, 0, 256))
-        act(a("chs"), P2, AF.Sign, scale=-1.0)
+        fs, PD = slot("fs", t), ps(pair_of[("s", t)], 256)
+        at("ae")
+        act(a("ae"), PD, AF.Abs, bias=-0.5)
+        at("pc")
+        mms(B1, [(blk, a("ad")), (a("b17"), a("ae")), (mat(E8), fs)])
+        at("ch")
+        act(a("chs"), B1, AF.Relu, bias=-144.25)
+        at("tt")
+        tt(a("tt4"), fs, PD, OP.mult)
+        at("px")
+        mms(C1, [(one, a("cv", CQ, CQ + 256, p=P0)), (mat(Q1), xt(t, m, NV, ST)), (mat(Q3), yv), (mat(Q1), a("tt4"))])
+        at("wn")
+        ts(wn(t, 0, 256), C1, 1.5 * 2 ** 23, OP.add, -1.5 * 2 ** 23, OP.add)
+        at("cp")
+        gcp(xt(t + 1, m, NV, ST), wn(t, 0, 256))
         if t < RO - 1:
-            act(xt(t, m, NV, ST), wn(t, 0, 256))
+            gcp(xt(t, m, NV, ST), wn(t, 0, 256))
 
     def count_changes(t):
-        old = a("fo") if t < 3 else slot("fd", t - 3)
-        mmg([(P2, a("eye"), slot("fd", t)), (P2, mat(NEG), old)])
-        act(a("ab"), P2, AF.Abs, scale=2.0 ** -18, acc=a("cnt", 0, 1))
-        mm(PA, a("cnm"), a("cnt", 0, 1), True, True)
-        ts(a("qi", 0, 1), PA, -31.5, OP.add, 1.0 / 64, OP.mult)
+        out = ps(3328, 256, p=P8)
+        old = (a("r8", 16, 24, p=P8), lanes("f8", t, p=P8)) if t < 3 else (a("r8", 8, 16), slot("fs", t - 3))
+        at("pn")
+        mms(out, [(a("r8", 0, 8), slot("fs", t)), old])
+        at("ab")
+        act(a("ab", p=P8), out, AF.Abs, bias=0.5 if t < 3 else 0.0, scale=0.5, acc=a("cnt", 0, 1, p=P8))
+        at("pa")
+        mm(PA, a("cnm", p=P33), a("cnt", 0, 1, p=P33))
+        at("qi")
+        ts(a("qi", 0, 1), PA, -2071.0, OP.add, 1.0 / 64, OP.mult)
+        at("am")
         ts(a("am", 0, 1), a("qi", 0, 1), -64.0, OP.mult, PA, OP.add)
 
-    def old_status(t):
-        ts(a("fo"), lanes("gt", t % 3), 200000.0, OP.is_gt, 64.0 * S, OP.mult)
-
     def final_status(t):
-        act(lanes("ff", t % 3), slot("fd", t), scale=2.0 ** -18)
+        out = ps(3328, 256, p=P8)
+        at("p8")
+        mm(out, a("r8", 0, 8), slot("fs", t))
+        at("ff")
+        act(lanes("ff", t % 3, p=P8), out, bias=0.5, scale=0.5)
 
-    def gat2(out, base, win, off, split):
+    def gat2(out, base, win, off, split, cap):
+        f = AF.Sign if cap else AF.Identity
         if split:
-            cp(a(out, base, base + 384), ind(win, a(off, 0, 24)))
-            act(a(out, base + 384, base + 768), ind(win, a(off, 24, 48)))
+            if cap:
+                ts(a(out, base, base + 384), ind(win, a(off, 0, 24)), 0.0, OP.is_gt)
+            else:
+                cp(a(out, base, base + 384), ind(win, a(off, 0, 24)))
+            act(a(out, base + 384, base + 768), ind(win, a(off, 24, 48)), f)
         else:
-            act(a(out, base, base + 768), ind(win, a(off)))
+            act(a(out, base, base + 768), ind(win, a(off)), f)
 
     def ghosts(t):
         last = t == RO - 1
-        gat2("hh", 0, a("chs"), "shu", last)
-        scan(a("cum"), a("rs5"), a("hh"), OP.mult, OP.add)
-        mmg([(PGO, one, row(CG, 48))] + [(PGO, sel("dgb", k), a("hh", k, 768, 16)) for k in range(16)] +
-            [(PGO, sel("dga", k), a("cum", k, 768, 16)) for k in range(16)])
-        tt(a("q48"), a("bas"), PGO, OP.min)
-        tt(a("r48"), a("q48"), a("shi"), OP.max)
+        at("hh")
+        gat2("hh", 0, a("chs"), "shu", last, True)
+        at("cum")
+        for d in range(3):
+            scan(slot("cum", d), slot("hh", d), a("cap"), OP.add, OP.min)
+        at("pg")
+        mms(PGO, [(eye, a("bs16"))] + [(sel("dgd", k), a("cum", k, 768, 16)) for k in range(16)] +
+            [(ps(3841 + 16 * d, 15), sel("dgd", 16), a("cum", 256 * d + 15, 256 * d + 255, 16)) for d in range(3)])
+        at("r48")
+        tt(a("r48"), a("shi"), PGO, OP.max)
+        at("o48")
         cp(a("o48"), a("r48"))
-        gat2("wn%d" % ((t + 1) % 2), 256, wn(t), "o48", last)
+        at("gw")
+        gat2("wn%d" % ((t + 1) % 2), 256, wn(t), "o48", last, False)
+        at("gh")
         exchange(t, -1, [wn(t + 1, 256 * (d + 1), 256 * (d + 2)) for d in range(3)],
                  [xt(t + 1, NV + 256 * d, NV + 256 * (d + 1)) for d in range(3)])
 
-    def origin_table(t):
-        cp(a("chi"), a("ci"))
-        mm(P3, a("eye"), a("chi"), True, True)
-        tt(a("clo"), a("ci"), P3, OP.subtract)
-        m = t % 3
-        dma("Y", "ot_%d" % t, ot(t, 256, 4352, p=R0), a("chi"))
-        dma("Y", "ot_%d" % t, ot(t, 256, 4352, p=R1), a("clo"))
-        dma("Y", "ot_%d" % t, ot(t, 0, 256, p=R1), a("vb", 256 * m, 256 * (m + 1), p=R1))
-
-    def origin_place(t):
-        act(half("kb", t), a("fra"), bias=256.0 - 2.0 ** 29, scale=-8192.0)
-        mmg([(P3, one, row(CI, 256)), (P3, a("eye"), half("kb", t))])
-        cp(half("oo", t), P3)
-
-    def gat_o(t, c):
-        act(ch("og", c), ind(ot(t), half("oo", t, 64 * c, 64 * (c + 1))))
-
-    def origins(t):
-        mmg([(P3, sel("slo", k), a("og", k, 4096, 16)) for k in range(16)])
-        if t < 2:
-            cp(half("o16", t), P3)
-            tt(half("dov", t), P3, half("vt", t), OP.subtract)
-            ts(P3, half("dov", t), 0.0, OP.not_equal)
-            tt(half("dkm", t), half("dkn", t), P3, OP.mult)
-        elif t == 2:
-            act(a("yob"), P3)
-        else:
-            tt(a("yob"), a("yob"), P3, OP.add)
-
-    def kept_origin(t):
-        tt(P2, half("kb", t), half("frn", t - 3), OP.is_equal)
-        tt(P2, half("dov", t - 3), P2, OP.mult)
-        tt(a("yob"), a("yob"), P2, OP.add)
-
     for q in range(16):
         j, h = q % 8, q // 8
-        if q == 12:
-            entries(0, lanes("ktb", 0), 0.0)
-        tt(a("gt", 192 * q, 192 * (q + 1)), a("ktb", 192 * q, 192 * (q + 1)), a("ps", 512 * j + 192 * h, 512 * j + 192 * (h + 1)), OP.add)
-    w2(0, 0), w2(0, 1), w2(0, 2)
+        at("gt%d", sum(q >= c for c in CUTS) - 1)
+        tt(a("gt", 192 * q, 192 * (q + 1)), a("ktb", 192 * q, 192 * (q + 1)), ps(512 * j + 192 * h, 192), OP.min)
+    for lo in (0, 128):
+        for t in range(3):
+            entries(t, lanes("ktb", t, lo, lo + 128), lo, lo + 128)
 
     for t in range(RO):
-        u = t - 1
+        now[1] = t
         if t >= 3:
-            gat_f(t, 0), gat_f(t, 1, TUNE["fv"] > 1), gat_f(t, 2), gat_f(t, 3, TUNE["fv"] > 0)
-            new_x(u)
             give_back(t)
-            w2(t, 0), w2(t, 1), w2(t, 2)
-            ghosts(u)
-            origin_table(t)
-        elif t > 0:
-            new_x(u)
-            ghosts(u)
-        else:
-            late_constants()
-            origin_table(0)
+        w2(t, 0), w2(t, 1), w2(t, 2)
         for c in range(4):
             gat_g(t, c)
         zr(t, 0)
         zr(t, 1)
-        flag(0)
-        if t > 0:
-            count_changes(u)
+        own_key(t, 0)
         scan2(t, 0)
         w2(t, 3)
-        own_key(t, 0)
         scan2(t, 1)
         winners(t, 0)
         w3(t, 0)
         gat_x(t, 0), gat_x(t, 1)
         zr(t, 2)
         zr(t, 3)
-        flag(1)
+        own_key(t, 1)
         scan2(t, 2)
         w3(t, 1)
-        own_key(t, 1)
         scan2(t, 3)
         winners(t, 1)
-        origin_place(t)
         w3(t, 2)
         gat_x(t, 2), gat_x(t, 3)
-        min3(t, 0)
+        min3(t, 0), min3(t, 1)
         w3(t, 3)
-        min3(t, 1)
-        scan3(0)
-        scan3(1)
-        if t < 3:
-            old_status(t)
-        if t < 2:
-            entries(t + 1, lanes("ktb", t + 1), 0.0)
+        min3(t, 2), min3(t, 3)
+        for c in range(4):
+            scan3(t, c)
+        at("yk")
         if t == 3:
-            tt(a("ykb"), slot("kp", 2), slot("kp", 3), OP.add)
-            act(a("yka"), a("ykb"), bias=-48.0 * S)
+            tt(a("yka"), slot("kp", 2), slot("kp", 3), OP.add)
         if t == 4:
-            kept_origin(3)
             tt(a("ykb"), a("yka"), slot("kp", 4), OP.add)
             dma("Y", "oyk", hbm(T.yk[:]), a("ykb"))
-        if t > 0:
-            for c in range(4):
-                gat_o(u, c)
-        if t < 2:
-            origin_table(t + 1)
-        min3(t, 2)
-        if t < 2:
-            w2(t + 1, 0)
-        scan3(2)
-        min3(t, 3)
-        if t < 2:
-            w2(t + 1, 1), w2(t + 1, 2)
-        scan3(3)
-        if t > 0:
-            origins(u)
+        pick(t, 0)
+        pick(t, 1)
         status(t)
+        new_x(t)
+        unpack(t)
+        if t < RO - 1:
+            count_changes(t)
         if t >= 2:
             final_status(t)
-    t = RO - 1
-    dma("Y", "oyf", hbm(T.yf[:]), a("ff", p=R0))
-    new_x(t)
-    dma("Y", "oyx", hbm(T.yx[:, 0:NV]), xt(t + 1, 0, NV), 790)
-    ghosts(t)
-    for c in range(4):
-        gat_o(t, c)
-    kept_origin(t)
-    origins(t)
-    dma("Y", "oyo", hbm(T.yo[:]), a("yob"))
-    dma("S", "oyg", hbm(T.yx[:, NV:NW]), xt(t + 1, NV, NW), 200)
-    ops.append({"q": "Y", "fn": None, "w": [], "r": [], "grp": None, "final": True, "hold": 0.0, "late": 0.0})
+        if t == RO - 1:
+            at("yf")
+            dma("Y", "oyf", hbm(T.yf[:]), a("ff", p=P8))
+            at("yx")
+            dma("Y", "oyx", hbm(T.yx[:, 0:NV]), xt(t + 1, 0, NV), 790)
+        ghosts(t)
+        if t < 2:
+            keep_origins(t)
+    at("end")
+    dma("S", "oyg", hbm(T.yx[:, NV:NW]), xt(RO, NV, NW), 200)
+    ops.append({"q": "Y", "fn": None, "w": [], "r": [], "grp": None, "final": True, "hold": 0.0, "late": 0.0, "tag": tuple(now)})
     _emit(g, T, _arrange(ops))

from concourse.bass import DstId, RemoteDMATransfer
from concourse.mybir import AluOpType as OP, ActivationFunctionType as AF

N, NV, NW, NL, ST, RO = 4, 3072, 3840, 256, 12, 5
S = 4096
BIG = 2.0 ** 24
CUTS = (0, 4, 8, 12, 15, 16)
F32, BF, I32, U16, F16 = "float32", "bfloat16", "int32", "uint16", "float16"


def _sb(n, d):
    return ("sbuf", [128, n], d)


SCRATCH = {
    "ps": ("psum", [128, 4096], F32),
    "ktb": _sb(NV, I32), "gt": _sb(NW, F32), "xt0": _sb(NW, BF), "xt1": _sb(NW, BF),
    "fst": _sb(192, I32), "f2": _sb(384, BF), "ffl": _sb(192, F32), "ff": _sb(NV, F32), "fb": _sb(192, BF), "f8": _sb(NV, BF),
    "thi": _sb(48, I32), "thc": _sb(48, F16), "thf": _sb(768, F16), "shi": _sb(48, I32), "shu": _sb(48, U16),
    "gg": _sb(4096, F32), "zz": _sb(4096, BF), "rr": _sb(4096, BF), "so": _sb(4096, F32),
    "xg": _sb(4096, BF), "t3": _sb(4096, BF), "s3": _sb(4096, BF), "so2": _sb(2048, F32),
    "pi": _sb(4, I32), "col": _sb(16, F32), "q128": _sb(128, F32), "qg": _sb(128, F32), "m16": _sb(17, F32), "m8": _sb(8, F32),
    "rev": _sb(8, F32), "c8": _sb(16, F32), "r8": _sb(24, BF), "md": _sb(16, F32), "thm": _sb(128, BF), "bks": _sb(128, BF),
    "eye": _sb(128, BF), "blk": _sb(128, BF), "b17": _sb(128, BF), "bs16": _sb(48, F16), "mats": _sb(9 * 128, BF),
    "sw2": _sb(1024, BF), "sw3": _sb(1024, BF), "dgd": _sb(17 * 128, BF), "csel": _sb(1024, BF),
    "cnm": _sb(128, F32), "lc": _sb(384, BF), "cv": _sb(1536, BF), "vv": _sb(768, BF),
    "rs2": _sb(1024, BF), "rs3": _sb(1024, BF), "cap": _sb(256, BF), "bas": _sb(48, F32), "zt": _sb(256, BF),
    "ci": _sb(768, I32), "c16": _sb(5 * 256, U16), "cf": _sb(5 * 256, F16), "kf": _sb(5 * 256, F32), "w2a": _sb(5 * 512, BF),
    "w2b": _sb(512, BF), "kp": _sb(5 * 256, I32), "kin": _sb(256, I32), "t1": _sb(256, F32),
    "cj": _sb(256, I32), "d16": _sb(256, U16), "fra": _sb(256, F32), "uu": _sb(256, BF),
    "xa": _sb(256, F32), "x1": _sb(256, F32), "x3": _sb(256, I32), "og": _sb(5 * 256, I32), "o16": _sb(512, U16), "of": _sb(512, F16),
    "ne": _sb(512, BF), "rs": _sb(512, BF), "fs": _sb(5 * 256, BF), "ad": _sb(256, BF), "ae": _sb(256, BF),
    "tt4": _sb(256, BF), "wn0": _sb(1024, BF), "wn1": _sb(1024, BF), "chs": _sb(256, BF), "hh": _sb(768, BF), "cum": _sb(768, BF),
    "r48": _sb(48, F32), "o48": _sb(48, U16),
    "ab": _sb(256, BF), "cnt": _sb(4, F32), "qi": _sb(4, I32), "am": _sb(4, F32),
    "yob": _sb(256, F32), "yoa": _sb(256, F32), "ykb": _sb(256, F32), "yka": _sb(256, F32),
}
DMA_GROUPS = ["lf", "lk0", "lk1", "lk2", "lk3", "lk4", "lt", "ls", "lxg", "lx0", "lx1", "dff", "df8", "dth", "oyx", "oyg", "oyf", "oyk", "oyo"]
SEMAPHORES = (["eV", "eS", "eP", "eG"] + DMA_GROUPS + ["snd%d" % t for t in range(RO + 1)] + ["arr%d" % t for t in range(RO + 1)])

TUNE = {"gather": 1.4, "hop": 40.0, "fv": {3: (1, 3), 4: (1, 3)}, "gv": {0: (1,)}, "xv": {},
        "rs": {t: (2, 3) for t in range(RO)}, "dg": (), "eg": (1, 2),
        "cv": ("c0", "c2", "c5", "c7", "c8", "c9", "c10", "c11")}
PLAN = {
    "V0": "c0 c2 c1 gt0 e00 gt1 gt2 e10 gt3 gt4 e20 e01 G1 Z0 e11 R0 c8 Z1 S0 R1 Z2 Z3 S1 b0 c9 kp0 cj0 c5 d0 fr0 c7 f20 S2 S3 "
          "f11 b1 kp1 e21 cj1 f10 d1 M0 fr1 c11 M1 M2 T0 T1 M3",
    "S0": "c4 c6 c14 e00 G0 e01 G2 G3 c3 zt0 c12 R2 wb0 R3 X0 uu0 f20 zt1 X1 wb1 X2 f10",
    "P0": "c0 W0 W1 W2 A0 D0 A1 K0 W3 D1 A3 J0 A2 D2 D3 K1 J1",
    "V1": "T2- T3- U0- U1- sc- gt- tt- x1- x2- wn- x4- Z0 cum- f21- R0 og- r48- o48- Z1 R1 c10- S0 Z2 Z3 qi- S1 am- b0 kp0 of- "
          "cj0 d0 S2 fr0 S3 ne- b1 kp1 cj1 fr1 M0 d1 M1 T0 T1 M2 M3",
    "S1": "X3- uu1- f11- c13- ad- ae- fs- xa- ch- G0 hh- G1 gw- G2 G3 ab- zt0 R2 R3 wb0 X0 zt1 X1 wb1 f21- uu0 X2",
    "P1": "V0- V1- V2- P1- P0- V3- P3- P2- pd- pb- W0 pf- pc- k1- px- pn- W1 W2 A0 pg- D0 A1 D1 W3 K0 pa- A2 A3 J0 D2 D3 K1 pv- J1",
    "V3": "T2- T3- U0- U1- sc- gt- tt- F1 F3 q0 x1- x2- wn- q1 cum- t1 t2 kin kf ci gb c16 x3- r48- x4- og- cf o48- qi- Z0 R0 Z1 "
          "R1 S0 Z2 Z3 S1 am- b0 kp0 cj0 d0 S2 fr0 S3 b1 kp1 cj1 d1 M0 fr1 M1 T0 M2 T1 M3",
    "S3": "X3- uu1- ad- ae- fs- xa- F0 ch- F2 hh- ab- rs wa G0 G1 gw- G2 G3 R2 zt0 R3 ff- wb0 X0 zt1 X1 wb1 uu0 X2",
    "P3": "V0- V1- V2- P0- P1- V3- P3- P2- pd- pb- k1- pf- pc- px- k2- Q0 H0 Q1 pq H1 pn- pa- pg- p8- W0 W1 W2 A0 D0 A1 D1 W3 K0 "
          "A2 A3 J0 D2 D3 K1 J1",
    "V5": "T2- T3- U1- tt- yk-- hh- wn- cum- yk- r48- o48- gw- U0- sc- x1- x2- yo-- x3- x4- og- yo-",
    "S5": "X3- uu1- ad- ae- fs- ch- hh- gw- ff- xa- end-",
    "P5": "V0- V1- V2- P0- V3- P1- P2- P3- pd- pb- pc- px- pg- k1- p8- k2-",
    "G0": "c0 c1 g3 e10 g5 g1 x e20 g2 g8 g4 g6 e11 e21 g7",
    "N0": "x", "Y0": "load c7", "G5": "cp- gh-", "N5": "gh-", "Y5": "yk- yf- yx- yo- end-",
}
for _t in range(1, RO):
    PLAN["G%d" % _t], PLAN["N%d" % _t] = "cp- gh- o16-", "gh-"
for _q in "VSP":
    PLAN[_q + "2"], PLAN[_q + "4"] = PLAN[_q + "1"], PLAN[_q + "3"]
_ORDER = {}


def _meet(x, y):
    return x[1] < y[2] and y[1] < x[2] and x[4] < y[5] and y[4] < x[5] and (x[3] != y[3] or (x[1] - y[1]) % x[3] == 0)


def _arrange(ops):
    key = (len(ops), str(sorted(TUNE.items())), str(PLAN))
    if key in _ORDER:
        return [ops[n] for n in _ORDER[key]]
    units, of = [], []
    for n, o in enumerate(ops):
        if o.get("join"):
            units[-1].append(n)
        else:
            units.append([n])
        of.append(len(units) - 1)
    sent = {o["grp"]: of[n] for n, o in enumerate(ops) if o["grp"] is not None}
    pred = [set() for _ in units]
    hist = {}
    for n, o in enumerate(ops):
        u = of[n]
        for (regs, wr) in ((o["r"], False), (o["w"], True)):
            for x in regs:
                pred[u].update(of[m] for (m, y, wr2) in hist.get(x[0], []) if (wr or wr2) and _meet(x, y))
        if o["q"] == "N":
            pred[u].add(sent["snd" + o["grp"][3:]])
        if o.get("final"):
            pred[u].update(range(u))
        pred[u].discard(u)
        for (regs, wr) in ((o["r"], False), (o["w"], True)):
            for x in regs:
                h = hist.setdefault(x[0], [])
                if wr and not o.get("part"):
                    h[:] = [e for e in h if not (x[1] <= e[1][1] and e[1][2] <= x[2])]
                h.append((n, x, wr))
    hold = [sum(ops[n]["hold"] for n in us) for us in units]
    late = [ops[us[-1]]["late"] for us in units]
    move = [ops[us[0]].get("move", 0.0) for us in units]
    eng = [ops[us[0]]["q"] for us in units]
    banks = [set(b for n in us for x in ops[n]["r"] + ops[n]["w"] if x[0] == "ps" for b in range(x[1] // 512, (x[2] - 1) // 512 + 1))
             for us in units]
    _ORDER["graph"] = (units, pred, None, eng, banks, hold, late, move, ops)
    named = {}
    for u, us in enumerate(units):
        named.setdefault((eng[u],) + ops[us[0]]["tag"], []).append(u)
    queue = {q: [u for t in range(RO + 1) for name in PLAN.get("%s%d" % (q, t), "").split()
                 for u in named.get((q, name.rstrip("-"), t - name.count("-")), [])][::-1] for q in "VSPGYN"}
    assert sorted(u for us in queue.values() for u in us) == list(range(len(units)))
    hop = TUNE["hop"]
    start, end, free, held, moving, order = {}, {}, {}, {}, 0.0, []

    def when(u):
        t = max([start[p] if eng[p] == eng[u] == "P" else end[p] + hop for p in pred[u]] + [free.get(eng[u], 0.0)])
        return max([t] + [x for b in banks[u] for q, x in held.get(b, {}).items() if q != eng[u]])

    while len(start) < len(units):
        t, u = min((when(us[-1]), us[-1]) for us in queue.values() if us and all(p in start for p in pred[us[-1]]))
        queue[eng[u]].pop()
        start[u], free[eng[u]], end[u] = t, t + hold[u], t + hold[u] + late[u]
        if move[u]:
            moving = max(moving, t + 1300.0) + move[u]
            end[u] = moving + 500.0
        for b in banks[u]:
            held.setdefault(b, {})[eng[u]] = end[u] + hop
        order += units[u]
    _ORDER[key] = order
    return [ops[n] for n in order]


def _emit(g, T, ops):
    queues = {"V": g.vector, "S": g.scalar, "P": g.tensor, "G": g, "Y": g.sync}
    hist = {}
    total = {o["grp"]: o["inc"] for o in ops if o["grp"] is not None}
    known = {q: ({}, set()) for q in queues}
    after = {}
    gclock = {}
    waited = set()
    for n, o in enumerate(ops):
        q = o["q"]
        deps = set()
        for (regs, wr) in ((o["r"], False), (o["w"], True)):
            for x in regs:
                for (m, y, wr2) in hist.get(x[0], []):
                    p = ops[m]
                    same = p["q"] == q and p["grp"] is None and o["grp"] is None
                    if x[0] == "ps" and not same:
                        hit = x[1] // 512 <= (y[2] - 1) // 512 and y[1] // 512 <= (x[2] - 1) // 512
                    else:
                        hit = (wr or wr2) and _meet(x, y)
                    if hit and not (same and q == "P"):
                        deps.add(m)
        if o.get("final"):
            deps = set(m for m, p in enumerate(ops[:n]) if p["grp"] is not None and p["grp"] not in waited)
        o["waits"] = []
        if q != "N":
            ck, gs = known[q]
            for m in sorted(deps, reverse=True):
                p = ops[m]
                if p["grp"] is not None:
                    if p["grp"] in gs:
                        continue
                    o["waits"].append(("g", p["grp"]))
                    waited.add(p["grp"])
                    c2, g2 = gclock[p["grp"]]
                    gs.add(p["grp"])
                else:
                    if ck.get(p["q"], -1) >= m:
                        continue
                    o["waits"].append(("e", m))
                    p["sig"] = True
                    c2, g2 = after[m]
                for k, v in c2.items():
                    ck[k] = max(ck.get(k, -1), v)
                gs.update(g2)
            if o["grp"] is None:
                c = dict(ck)
                c[q] = n
                after[n] = (c, set(gs))
            else:
                gclock[o["grp"]] = (dict(ck), set(gs))
        else:
            gclock[o["grp"]] = ({}, set())
        for (regs, wr) in ((o["r"], False), (o["w"], True)):
            for x in regs:
                h = hist.setdefault(x[0], [])
                if wr and x[0] != "ps" and not o.get("part"):
                    h[:] = [e for e in h if not (x[1] <= e[1][1] and e[1][2] <= x[2])]
                h.append((n, x, wr))
    count = {}
    for o in ops:
        if o.get("sig"):
            count[o["q"]] = count.get(o["q"], 0) + 1
            o["cnt"] = count[o["q"]]
    for o in ops:
        if o["q"] == "N":
            continue
        e = queues[o["q"]]
        best = {}
        for kind, x in o["waits"]:
            if kind == "g":
                best[x] = total[x]
            else:
                s = "e" + ops[x]["q"]
                best[s] = max(best.get(s, 0), ops[x]["cnt"])
        for s, v in best.items():
            e.wait_ge(T.sem[s], v)
        if o["fn"] is None:
            continue
        ins = o["fn"](e)
        if o["grp"] is not None:
            if o["dma"]:
                ins.then_inc(T.sem[o["grp"]], 16)
        elif o.get("sig"):
            ins.then_inc(T.sem["e" + o["q"]], 1)


def rank_program(g, core, T, topo):
    rank = T.rank_of(core)
    if rank is None:
        return
    ops = []
    now = ["load", 0]

    def at(name, *k):
        now[0] = name % k

    def a(name, lo=0, hi=None, st=1, p=None):
        t = T[name]
        hi = t.shape[1] if hi is None else hi
        ap = t[slice(None) if p is None else p, slice(lo, hi) if st == 1 else slice(lo, hi, st)]
        return (ap, [(name, lo, hi, st) + ((0, 128) if p is None else (p.start, p.stop))], st != 1 or p is not None,
                len(range(lo, hi, st)), SCRATCH[name][2])

    def ind(win, off):
        return (win[0].indirect(off[0]), win[1] + off[1], False, 0, win[4])

    def hbm(ap):
        return (ap, [], False, 2, None)

    def val(x):
        return x[0] if isinstance(x, tuple) else x

    def regs(*xs):
        out = []
        for x in xs:
            if isinstance(x, tuple):
                out += x[1]
        return out

    def op(q, fn, outs, ins, grp=None, inc=16, dma=True, rate=None, **more):
        o = {"q": q, "fn": fn, "w": regs(*outs), "r": regs(*ins), "grp": grp, "inc": inc, "dma": dma,
             "part": any(x[2] for x in outs), "hold": 0.0, "late": 0.0, "tag": tuple(now)}
        big = [x for x in ins if isinstance(x, tuple) and x[3] != 1]
        if grp is not None:
            o["hold"], o["late"] = (60.0, 2500.0) if dma else ((500.0, 3000.0) if q == "G" else (0.0, 500.0))
        elif q == "P":
            o["hold"], o["late"] = 5 + 0.44 * max(64, outs[0][3]) * (4 if ins[0][4] == F32 else 1), 50.0
        elif q == "G":
            o["hold"], o["late"] = 150 + 1.66 * outs[0][3], 400.0
        elif any(x[3] == 0 for x in big):
            o["gn"] = outs[0][3]
            o["hold"] = 60 + 0.83 * TUNE["gather"] * outs[0][3]
        else:
            if rate is None:
                rate = 0.5 if q == "V" and all(x[4] in (BF, U16, F16) for x in big + [outs[0]]) else 1.0
            o["hold"] = (30 if q == "V" else 105) + 0.83 * max(64, rate * outs[0][3])
        o.update(more)
        ops.append(o)

    def tt(out, x, y, o):
        op("V", lambda e: e.tensor_tensor(out[0], x[0], y[0], o), [out], [x, y],
           rate=1.0 if "ps" in (x[1][0][0], y[1][0][0]) else 2.0)

    def ts(out, x, s1, o0, s2=None, o1=None):
        if o1 is None:
            op("V", lambda e: e.tensor_scalar(out[0], x[0], val(s1), None, o0), [out], [x, s1])
        else:
            op("V", lambda e: e.tensor_scalar(out[0], x[0], val(s1), val(s2), o0, o1), [out], [x, s1, s2])

    def cp(out, x):
        op("V", lambda e: e.tensor_copy(out[0], x[0]), [out], [x])

    def ms(out, c):
        op("V", lambda e: e.memset(out[0], c), [out], [])

    def scan(out, d0, d1, o0, o1, first=0.0):
        op("V", lambda e: e.tensor_tensor_scan(out[0], d0[0], d1[0], first, o0, o1), [out], [d0, d1])

    def act(out, x, f=AF.Identity, bias=0.0, scale=1.0, acc=None):
        if acc is None:
            op("S", lambda e: e.activation(out[0], x[0], f, bias=val(bias), scale=val(scale)), [out], [x, bias, scale])
        else:
            op("S", lambda e: e.activation(out[0], x[0], f, bias=val(bias), scale=val(scale), accum_out=acc[0]), [out, acc], [x, bias, scale])

    def gcp(out, x):
        op("G", lambda e: e.affine_select(out[0], x[0], [[0, out[3]]], OP.is_ge, 0.0, 0, 0), [out], [x])

    def mm(out, l, r, start=True, stop=True, **more):
        op("P", lambda e: e.matmul(out[0], l[0], r[0], start, stop), [out], [l, r], **more)

    def mms(out, items):
        for j, x in enumerate(items):
            mm(*((out,) + x)[-3:], j == 0, j == len(items) - 1, join=j > 0)

    def iota(out, pat, base=0, cm=0, small=True):
        if small:
            op("G", lambda e: e.iota(out[0], pat, base, cm, allow_small_or_imprecise_dtypes=True), [out], [])
        else:
            op("G", lambda e: e.iota(out[0], pat, base, cm), [out], [])

    def dma(q, grp, out, x, kb=60):
        op(q, lambda e: e.dma_start(out[0], x[0]), [out], [x], grp, move=3.4 * kb)

    def masks(src, dsts):
        sets = [topo.engines(src, d) for d in dsts]
        narrow = min(sets, key=len)
        tight = [j for j, s in enumerate(sets) if len(s) == len(narrow)]
        wide = [j for j in range(len(dsts)) if j not in tight]
        out = {}
        for group, pool in ((tight, narrow), (wide, [e for e in max(sets, key=len) if e not in narrow])):
            if group:
                n = 1
                while 2 * n * len(group) <= len(pool):
                    n *= 2
                for i, j in enumerate(group):
                    out[j] = pool[i * n:(i + 1) * n]
        return [out[j] for j in range(len(dsts))]

    def exchange(tag, sign, srcs, dsts):
        to = [T.cores[(rank + sign * (1 + d)) % N] for d in range(N - 1)]
        eng = masks(core, to)
        tr = []
        for d in range(N - 1):
            rid, pid, _ = topo.addr(to[d])
            tr.append(RemoteDMATransfer(dst_ids=[DstId(rid=rid, pnc=pid)], dma_engine_mask=sum(1 << e for e in eng[d]),
                                        remote_sem=T.sem["arr%d" % tag], src=srcs[d][0], dst=dsts[d][0]))
        op("G", lambda e: e.remote_dma_fused(tr, local_sem=T.sem["snd%d" % tag]), [], srcs, "snd%d" % tag, sum(len(x) for x in eng), False)
        got = 0
        for d in range(N - 1):
            r = (rank - sign * (1 + d)) % N
            got += len(masks(T.cores[r], [T.cores[(r + sign * (1 + k)) % N] for k in range(N - 1)])[d])
        op("N", None, dsts, [], "arr%d" % tag, got, False)

    P0, P8, P33, P97 = slice(0, 1), slice(0, 8), slice(0, 33), slice(0, 97)
    part = lambda r: slice(r, r + 1)
    col = lambda j: a("col", j, j + 1)
    mat = lambda j: a("mats", 128 * j, 128 * (j + 1))
    sel = lambda name, j, **kw: a(name, 128 * j, 128 * (j + 1), **kw)
    MATS = [-1.0, 2048.0, BIG, 64.0 * S, 0.25, 0.75, 8.25, float(S), -2048.0]
    NEG, T2K, PB, FLAG, Q1, Q3, E8, K4K, N2K = range(len(MATS))
    PP, PM, PG, H0, H1, SC0, SC1, BB0, BB1, BK0, BK1, FS0, FS1, FB0, FB1 = range(15)
    CD, CO, CB, CQ = 0, 512, 1024, 1280
    one, ones = a("lc", 0, 128, p=P0), a("lc", 0, 128, p=P97)
    eye, blk = a("eye"), a("blk")
    xt = lambda t, *k: a("xt%d" % (t % 2), *k)
    wn = lambda t, *k: a("wn%d" % (t % 2), *k)
    slot = lambda name, t, lo=0, hi=256, **kw: a(name, 256 * t + lo, 256 * t + hi, **kw)
    lanes = lambda name, m, lo=0, hi=256, **kw: a(name, m + ST * lo, ST * hi, ST, **kw)
    ch = lambda name, c: a(name, 1024 * c, 1024 * (c + 1))
    ps = lambda lo, n, **kw: a("ps", lo, lo + n, **kw)
    pair_of = {}
    x, y, z = 0, 1024, 2048
    for t in range(RO):
        if t >= 3:
            pair_of["q", t] = x
            x, y, z = y, z, x
        for key, lo in ((("a", 0), x), (("a", 1), y), (("a", 2), z), (("a", 3), x), (("b", 0), y), (("b", 1), z), (("b", 2), x),
                        (("o", 0), y), (("b", 3), z), (("o", 1), x)):
            pair_of[key[0], t, key[1]] = lo
        pair_of["s", t] = z
        x, y = y, x
    take = lambda key: pair_of[key]

    pp = lambda key: ps(pair_of[key], 1024)
    B0, B1, C1 = ps(3072, 256), ps(3328, 256), ps(3840, 256)
    PA, PGO = ps(3072, 1), ps(3840, 48)
    KEY, TURN = (3584, 3200), (3712, 3072)
    yv = a("s3", 15, 4096, 16)

    def diagonal(lo, name, h):
        for k in range(16):
            mm(a("ps", lo + k, lo + 128, 16), a(name, 2048 * h + k, 2048 * (h + 1), 16), a("eye", k, 128, 16), join=k % 8 > 0)

    dma("Y", "lf", a("fst"), hbm(T.f0[:]))
    for j in range(len(CUTS) - 1):
        lo, hi = 192 * CUTS[j], 192 * CUTS[j + 1]
        dma("Y", "lk%d" % j, a("ktb", lo, hi), hbm(T.kt[:, lo:hi]), (hi - lo) // 2)
    dma("Y", "lxg", a("xt0", NV, NW), hbm(T.x0[:, NV:NW]), 200)
    dma("Y", "lt", a("thi"), hbm(T.th[:]))
    dma("Y", "ls", a("shi"), hbm(T.shw[:]))
    dma("Y", "lx0", a("xt0", 0, NV), hbm(T.x0[:, 0:NV]), 790)
    dma("Y", "lx1", a("xt1", 0, NV), hbm(T.x0[:, 0:NV]), 790)

    def put(out, c):
        if now[0] in TUNE["cv"]:
            ms(out, c)
        else:
            act(out, out, bias=c, scale=0.0)

    def times(out, x, c):
        if now[0] in TUNE["cv"]:
            ts(out, x, c, OP.mult)
        else:
            act(out, x, scale=c)

    at("c0")
    iota(a("pi", 0, 1), [[0, 1]], 0, 1, False)
    iota(a("qg"), [[1, 8], [0, 16]])
    iota(a("q128"), [[1, 128]])
    iota(a("rev"), [[-1, 8]], 15)
    iota(a("gt", NV, NW), [[0, NW - NV]], -64 * S)
    ts(a("pi", 1, 2), a("pi", 0, 1), 15, OP.bitwise_and)
    ts(a("pi", 2, 3), a("pi", 0, 1), 4, OP.arith_shift_right)
    cp(a("col", PP, PG + 1), a("pi", 0, 3))
    ts(blk, a("qg"), col(PG), OP.is_equal)
    ts(a("m16"), a("q128", 0, 17), col(PM), OP.is_equal)
    ts(col(H0), col(PM), 7.5, OP.is_lt)
    ts(col(H1), col(PM), 7.5, OP.is_gt)
    tt(a("m8"), a("m16", 0, 8), a("m16", 8, 16), OP.add)
    ts(a("bks"), blk, float(S), OP.mult)
    ts(eye, a("q128"), col(PP), OP.is_equal)
    hh2 = a("col", H0, H1 + 1)
    ts(a("col", FS0, FS1 + 1), hh2, 128.0, OP.mult)
    ts(a("col", FB0, FB1 + 1), hh2, -64.0, OP.mult)
    ts(a("col", SC0, SC1 + 1), hh2, 1.0 / S, OP.mult)
    ts(a("col", BK0, BK1 + 1), hh2, 159.0625, OP.mult, 0.46875, OP.add)
    for j in range(8):
        times(sel("sw2", j), a("bks"), a("m8", j, j + 1))
    for h in range(2):
        ts(a("f2", 192 * h, 192 * (h + 1)), a("fst"), col(FS0 + h), OP.mult, col(FB0 + h), OP.add)
    for j in range(8):
        mm(ps(512 * j, 384), sel("sw2", j), a("f2"))
    at("c1")
    ts(a("col", BB0, BB1 + 1), hh2, 512.0, OP.mult, -240.0, OP.add)
    ts(a("c8", 0, 8), a("m16", 0, 8), -float(S), OP.mult)
    ts(a("rev"), a("rev"), col(PM), OP.is_equal)
    tt(a("md"), a("m16", 1, 17), a("m16", 0, 16), OP.subtract)
    ts(a("thm"), a("qg"), col(PP), OP.is_equal, -1.0, OP.mult)
    tt(a("c8", 8, 16), a("c8", 0, 8), a("rev"), OP.subtract)
    iota(a("lc"), [[0, 384]])
    iota(a("cv", CD, CO), [[0, CO - CD]])
    for lo, scales in ((0, (1, 1, S, S * S // 2)), (128, (1, 1, 1, S // 2)), (256, (-1, -1))):
        at("c14" if lo == 0 else "c8")
        for r, c in enumerate(scales):
            put(a("lc", lo, lo + 128, p=part(32 * r)), float(c))
    at("c14")
    times(mat(NEG), eye, MATS[NEG])
    put(a("cv", CD, CO, p=part(32)), 1.0 / 32)
    for r, c in ((0, -1920.0), (32, -0.5), (64, -32.0)):
        put(a("cv", CD + 15, CO, 16, p=part(r)), c)
    at("c2")
    times(a("sw3"), a("sw2"), 17.0 / S)
    at("c3")
    for j in range(8):
        times(sel("csel", j), blk, a("c8", 8 + j, 9 + j))
    at("c4")
    for j in range(1, len(MATS)):
        times(mat(j), eye, MATS[j])
    times(a("b17"), blk, 17.0)
    at("c5")
    times(a("r8", 0, 8), a("blk", 0, 128, 16), a("m16", 0, 1))
    times(a("r8", 16, 24), a("eye", 0, 8), -2.0)
    times(a("r8", 8, 16), a("r8", 0, 8), -1.0)
    for k in range(17):
        at(("c6", "c12", "c13")[k // 6])
        times(sel("dgd", k), mat(T2K), a("md", k, k + 1) if k < 16 else a("m16", 0, 1))
    at("g1")
    gcp(a("ffl"), a("fst"))
    gcp(a("fb"), a("fst"))
    gcp(a("shu"), a("shi"))
    iota(a("bas"), [[16, 48]], 256)
    at("x")
    exchange(RO, 1, [a("xt0", NV + 256 * d, NV + 256 * (d + 1)) for d in range(3)],
             [a("wn0", 256 * (d + 1), 256 * (d + 2)) for d in range(3)])
    at("g2")
    iota(a("rs3"), [[0, 1024]], 1)
    iota(a("rs3", 0, 1024, 16), [[0, 64]])
    at("g3")
    iota(a("cv", CO, CB), [[0, 64], [4, 8]], -30)
    at("g4")
    iota(a("cv", CB, CQ + 256), [[0, CQ + 256 - CB]], -34)
    at("c9")
    for r, c in ((0, -1920.0), (32, 0.0), (64, -1920.0)):
        put(a("cv", CO, CB, p=part(r)), c)
    at("c10")
    for r, c in ((0, 0.0), (32, 0.0), (64, -128.0)):
        put(a("cv", CB, CQ, p=part(r)), c)
    at("g5")
    iota(a("rs2"), [[0, 1024]], -1)
    iota(a("rs2", 0, 1024, 8), [[0, 128]])
    at("g6")
    iota(a("vv"), [[1, 3], [0, 16], [12, 16]])
    at("g7")
    iota(a("vv", p=P0), [[0, 3], [192, 16], [0, 16]], -1920)
    at("c11")
    put(a("vv", p=part(64)), 1920.0)
    put(a("vv", p=part(96)), -34.0)
    at("g8")
    iota(a("cap"), [[0, 256]], 64)
    iota(a("cnm"), [[0, 128]], 1)
    iota(a("cnt"), [[0, 4]])
    at("c7")
    put(a("cnt", 0, 1, p=part(32)), 2039.5)
    ts(a("thc"), a("thi"), -2040.0, OP.add)
    ts(a("bs16"), a("bas"), col(PM), OP.add)
    put(a("cv", CQ, CQ + 256, p=P0), -0.25)
    dma("Y", "dff", a("ff", p=P8), a("ffl"))
    dma("Y", "df8", a("f8", p=P8), a("fb"), 30)
    dma("Y", "dth", a("thf", p=P8), a("thc"), 30)

    def entries(t, src, lo, hi):
        name = lambda x: at(x) if t >= 3 else at("e%d%d", t, lo // 128)
        name("ci")
        cast = gcp if t in TUNE["eg"] else cp
        ts(slot("ci", t % 3, lo, hi), src, S - 1, OP.bitwise_and)
        if t < 3:
            cast(slot("kf", t, lo, hi), src)
        name("c16")
        cast(slot("c16", t, lo, hi), slot("ci", t % 3, lo, hi))
        if t in (1, 2):
            name = lambda x: at("f%d%d", t, lo // 128)
        name("cf")
        ts(slot("cf", t, lo, hi), slot("c16", t, lo, hi), -1920.0, OP.add)
        name("wa")
        for h in range(2):
            act(a("w2a", 512 * t + 2 * lo + h, 512 * t + 2 * hi, 2), slot("kf", t, lo, hi), bias=col(BK0 + h), scale=col(SC0 + h))

    def gather(name, key, t, c, win, off):
        at({"fv": "F%d", "gv": "G%d", "xv": "X%d"}[key], c)
        (cp if c in TUNE[key].get(t, ()) else act)(ch(name, c), ind(win, off))

    def give_back(t):
        u = t - 3
        for c in range(4):
            gather("xg", "fv", t, c, a("gt"), slot("o16", u, 64 * c, 64 * (c + 1)))
        lo = take(("q", t))
        Q, T2, PF = ps(lo, 256), ps(lo + 512, 256), ps(lo + 768, 256)
        at("pq")
        mm(PF, mat(FLAG), slot("fs", u))
        for h in range(2):
            at("Q%d", h)
            diagonal(lo + 256 + 128 * h, "xg", h)
            at("q%d", h)
            ts(sel("zt", h), ps(lo + 256 + 128 * h, 128), 0.0, OP.is_ge, 0.5, OP.subtract)
            at("H%d", h)
            mms(ps(lo + 128 * h, 128), [(mat(FLAG), slot("ne", u, 128 * h, 128 * (h + 1))), (sel("zt", h), mat(FLAG))])
        at("t1")
        tt(a("t1"), slot("kp", u), Q, OP.min)
        at("t2")
        tt(T2, slot("kf", u), Q, OP.subtract)
        at("rs")
        act(slot("rs", u), Q, AF.Sign, bias=-1.0)
        at("kin")
        tt(a("kin"), a("t1"), T2, OP.max)
        at("gb")
        tt(lanes("gt", t % 3), a("kin"), PF, OP.min)
        at("kf")
        tt(slot("kf", t), a("t1"), T2, OP.max)
        entries(t, a("kin"), 0, 256)

    def weights(key, name, rhs, base, c):
        at("W%d" if key[0] == "a" else "V%d", c)
        take(key)
        for b in range(2):
            lo = pair_of[key] + 512 * b
            for j in range(8):
                mm(a("ps", lo + j, lo + 512, 8), sel(name, j), a(rhs, base + 128 * c + 64 * b, base + 128 * c + 64 * (b + 1)), join=j > 0)

    w2 = lambda t, c: weights(("a", t, c), "sw2", "w2a", 512 * t, c)
    w3 = lambda t, c: weights(("b", t, c), "sw3", "w2b", 0, c)
    gat_g = lambda t, c: gather("gg", "gv", t, c, a("gt"), slot("c16", t, 64 * c, 64 * (c + 1)))
    gat_x = lambda t, c: gather("xg", "xv", t, c, xt(t), a("d16", 64 * c, 64 * (c + 1)))

    def zr(t, c):
        at("Z%d", c)
        tt(ch("zz", c), pp(("a", t, c)), ch("gg", c), OP.subtract)
        at("R%d", c)
        if c in TUNE["rs"].get(t, ()):
            act(ch("rr", c), ch("zz", c), AF.Relu, bias=160.0 * S, scale=-1.0)
            here, nxt = mat(NEG), eye
        else:
            ts(ch("rr", c), ch("zz", c), 160.0 * S, OP.min, 160.0 * S, OP.subtract)
            here, nxt = eye, mat(NEG)
        at("A%d", c)
        for b in range(2):
            mm(ps(pair_of[("a", t, c)] + 512 * b, 512), ones, a("cv", CD, CO, p=P97), True, False)
        at("D%d", c)
        for b in range(2):
            lo, x = pair_of[("a", t, c)] + 512 * b, 1024 * c + 512 * b
            mm(ps(lo, 512), here, a("rr", x, x + 512), False, False)
            mm(ps(lo, 511), nxt, a("rr", x + 1, x + 512), False, False)
            mm(a("ps", lo + 15, lo + 511, 16), here, a("rr", x + 16, x + 512, 16), False, True, join=True)

    def scan2(t, c):
        at("S%d", c)
        scan(ch("so", c), ch("gg", c), pp(("a", t, c)), OP.max, OP.add, -40.0 * S)

    def own_key(t, h):
        at("K%d", h)
        diagonal(TURN[h], "zz", h)
        at("zt%d", h)
        act(sel("zt", h), ps(TURN[h], 128), bias=-256.0 * S)
        at("J%d", h)
        mms(ps(KEY[h], 128), [(eye, slot("cf", t, 128 * h, 128 * (h + 1))), (sel("zt", h), eye)])

    def winners(t, h):
        lo, hi = 128 * h, 128 * (h + 1)
        b = ps(KEY[h], 128)
        at("b%d", h)
        tt(b, a("so", 2048 * h + 15, 2048 * (h + 1), 16), b, OP.max)
        at("kp%d", h)
        ts(slot("kp", t, lo, hi), b, 32.0 * S + 1920.25, OP.add)
        at("cj%d", h)
        ts(a("cj", lo, hi), slot("kp", t, lo, hi), S - 1, OP.bitwise_and)
        at("d%d", h)
        (gcp if h in TUNE["dg"] else cp)(a("d16", lo, hi), a("cj", lo, hi))
        at("fr%d", h)
        tt(a("fra", lo, hi), b, slot("kp", t, lo, hi), OP.subtract)
        at("wb%d", h)
        for j in range(2):
            act(a("w2b", 2 * lo + j, 2 * hi, 2), b, bias=col(BB0 + j), scale=col(SC0 + j))
        at("uu%d", h)
        act(a("uu", lo, hi), a("fra", lo, hi), AF.Abs, bias=2.0 ** 23 + 64 * 1920.5 - 15, scale=64.0)

    def min3(t, c):
        at("M%d", c)
        tt(ch("t3", c), ch("xg", c), pp(("b", t, c)), OP.min)

    def scan3(t, c):
        at("T%d", c)
        scan(ch("s3", c), a("rs3"), ch("t3", c), OP.mult, OP.max)

    def pick(t, h):
        base = take(("o", t, h))
        for b in range(2):
            at("P%d", 2 * h + b)
            lo, x = base + 512 * b, 128 * h + 64 * b
            mm(ps(lo, 512), ones, a("cv", CO, CO + 512, p=P97), True, False)
            for j in range(16):
                l, r = (mat(PB), a("uu", x, x + 64)) if j < 8 else (sel("csel", j - 8), slot("cf", t, x, x + 64))
                mm(a("ps", lo + j % 8, lo + 512, 8), l, r, False, j == 15, join=j % 8 > 0)
        at("U%d", h)
        scan(ch("so2", h), a("rs2"), ps(base, 1024), OP.mult, OP.min)

    def unpack(t):
        lo = pair_of[("s", t)]
        SC, K1, K2 = ps(lo + 512, 256), ps(lo + 768, 256), ps(lo + 256, 256)
        own = (a("lc", 128, 256, p=P97), slot("vv", t % 3, p=P97))
        at("sc")
        ts(SC, a("fra"), 15.0 / 64 - 32 * S - 1920.5, OP.is_lt, 1.0 / S, OP.max)
        at("k1")
        mms(K1, [own, (mat(K4K), a("uu"))] + ([(mat(N2K), slot("rs", t - 3)), (mat(N2K), a("rs3", 1, 1024, 4))] if t >= 3 else []))
        if t >= 3:
            at("k2")
            mms(K2, [(own[0], a("cv", CB, CQ, p=P97)), (mat(K4K), a("uu")), (mat(T2K), slot("rs", t - 3)), (eye, slot("of", t - 3))])
        at("xa")
        act(a("xa"), a("so2", 7, 2048, 8), AF.Abs)
        at("x1")
        tt(a("x1"), a("xa"), SC, OP.mult)
        at("x2")
        tt(a("x1"), a("x1"), K1, OP.max)
        if t >= 3:
            at("x3")
            tt(a("x1"), a("x1"), K2, OP.max)
        at("x4")
        ts(a("x3"), a("x1"), 2.0, OP.mult, -0.4375, OP.add)
        at("og")
        ts(slot("og", t), a("x3"), 1, OP.arith_shift_right, S - 1, OP.bitwise_and)
        at("yo")
        if t == 3:
            tt(a("yoa"), slot("og", 2), slot("og", 3), OP.add)
        if t == 4:
            tt(a("yob"), a("yoa"), slot("og", 4), OP.add)
            dma("Y", "oyo", hbm(T.yo[:]), a("yob"))

    def keep_origins(t):
        at("o16")
        gcp(slot("o16", t), slot("og", t))
        at("of")
        ts(slot("of", t), slot("o16", t), -1920.0, OP.add)
        at("pv")
        mms(C1, [(eye, slot("of", t)), (a("lc", 256, 384, p=P33), slot("vv", t, p=P33))])
        at("ne")
        ts(slot("ne", t), C1, 0.0, OP.is_equal, 0.5, OP.add)

    def status(t):
        m = t % 3
        PD = ps(take(("s", t)), 256)
        at("pd")
        mms(PD, [(mat(NEG), xt(t, m, NV, ST)), (eye, yv)])
        at("ad")
        act(a("ad"), PD, AF.Abs)
        at("pb")
        mms(B0, [(a("thm", p=P8), slot("thf", m, p=P8)), (blk, a("ad"))])
        at("fs")
        act(slot("fs", t), B0, AF.Sign, bias=2039.5 if t == 0 else a("am", 0, 1), scale=-1.0)
        if t < RO - 1:
            at("pf")
            mm(C1, mat(FLAG), slot("fs", t))
            at("gt")
            tt(lanes("gt", m), slot("kp", t), C1, OP.min)

    def new_x(t):
        m = t % 3
        fs, PD = slot("fs", t), ps(pair_of[("s", t)], 256)
        at("ae")
        act(a("ae"), PD, AF.Abs, bias=-0.5)
        at("pc")
        mms(B1, [(blk, a("ad")), (a("b17"), a("ae")), (mat(E8), fs)])
        at("ch")
        act(a("chs"), B1, AF.Relu, bias=-144.25)
        at("tt")
        tt(a("tt4"), fs, PD, OP.mult)
        at("px")
        mms(C1, [(one, a("cv", CQ, CQ + 256, p=P0)), (mat(Q1), xt(t, m, NV, ST)), (mat(Q3), yv), (mat(Q1), a("tt4"))])
        at("wn")
        ts(wn(t, 0, 256), C1, 1.5 * 2 ** 23, OP.add, -1.5 * 2 ** 23, OP.add)
        at("cp")
        gcp(xt(t + 1, m, NV, ST), wn(t, 0, 256))
        if t < RO - 1:
            gcp(xt(t, m, NV, ST), wn(t, 0, 256))

    def count_changes(t):
        out = ps(3328, 256, p=P8)
        old = (a("r8", 16, 24, p=P8), lanes("f8", t, p=P8)) if t < 3 else (a("r8", 8, 16), slot("fs", t - 3))
        at("pn")
        mms(out, [(a("r8", 0, 8), slot("fs", t)), old])
        at("ab")
        act(a("ab", p=P8), out, AF.Abs, bias=0.5 if t < 3 else 0.0, scale=0.5, acc=a("cnt", 0, 1, p=P8))
        at("pa")
        mm(PA, a("cnm", p=P33), a("cnt", 0, 1, p=P33))
        at("qi")
        ts(a("qi", 0, 1), PA, -2071.0, OP.add, 1.0 / 64, OP.mult)
        at("am")
        ts(a("am", 0, 1), a("qi", 0, 1), -64.0, OP.mult, PA, OP.add)

    def final_status(t):
        out = ps(3328, 256, p=P8)
        at("p8")
        mm(out, a("r8", 0, 8), slot("fs", t))
        at("ff")
        act(lanes("ff", t % 3, p=P8), out, bias=0.5, scale=0.5)

    def gat2(out, base, win, off, split, cap):
        f = AF.Sign if cap else AF.Identity
        if split:
            if cap:
                ts(a(out, base, base + 384), ind(win, a(off, 0, 24)), 0.0, OP.is_gt)
            else:
                cp(a(out, base, base + 384), ind(win, a(off, 0, 24)))
            act(a(out, base + 384, base + 768), ind(win, a(off, 24, 48)), f)
        else:
            act(a(out, base, base + 768), ind(win, a(off)), f)

    def ghosts(t):
        last = t == RO - 1
        at("hh")
        gat2("hh", 0, a("chs"), "shu", last, True)
        at("cum")
        for d in range(3):
            scan(slot("cum", d), slot("hh", d), a("cap"), OP.add, OP.min)
        at("pg")
        mms(PGO, [(eye, a("bs16"))] + [(sel("dgd", k), a("cum", k, 768, 16)) for k in range(16)] +
            [(ps(3841 + 16 * d, 15), sel("dgd", 16), a("cum", 256 * d + 15, 256 * d + 255, 16)) for d in range(3)])
        at("r48")
        tt(a("r48"), a("shi"), PGO, OP.max)
        at("o48")
        cp(a("o48"), a("r48"))
        at("gw")
        gat2("wn%d" % ((t + 1) % 2), 256, wn(t), "o48", last, False)
        at("gh")
        exchange(t, -1, [wn(t + 1, 256 * (d + 1), 256 * (d + 2)) for d in range(3)],
                 [xt(t + 1, NV + 256 * d, NV + 256 * (d + 1)) for d in range(3)])

    for q in range(16):
        j, h = q % 8, q // 8
        at("gt%d", sum(q >= c for c in CUTS) - 1)
        tt(a("gt", 192 * q, 192 * (q + 1)), a("ktb", 192 * q, 192 * (q + 1)), ps(512 * j + 192 * h, 192), OP.min)
    for lo in (0, 128):
        for t in range(3):
            entries(t, lanes("ktb", t, lo, lo + 128), lo, lo + 128)

    for t in range(RO):
        now[1] = t
        if t >= 3:
            give_back(t)
        w2(t, 0), w2(t, 1), w2(t, 2)
        for c in range(4):
            gat_g(t, c)
        zr(t, 0)
        zr(t, 1)
        own_key(t, 0)
        scan2(t, 0)
        w2(t, 3)
        scan2(t, 1)
        winners(t, 0)
        w3(t, 0)
        gat_x(t, 0), gat_x(t, 1)
        zr(t, 2)
        zr(t, 3)
        own_key(t, 1)
        scan2(t, 2)
        w3(t, 1)
        scan2(t, 3)
        winners(t, 1)
        w3(t, 2)
        gat_x(t, 2), gat_x(t, 3)
        min3(t, 0), min3(t, 1)
        w3(t, 3)
        min3(t, 2), min3(t, 3)
        for c in range(4):
            scan3(t, c)
        at("yk")
        if t == 3:
            tt(a("yka"), slot("kp", 2), slot("kp", 3), OP.add)
        if t == 4:
            tt(a("ykb"), a("yka"), slot("kp", 4), OP.add)
            dma("Y", "oyk", hbm(T.yk[:]), a("ykb"))
        pick(t, 0)
        pick(t, 1)
        status(t)
        new_x(t)
        unpack(t)
        if t < RO - 1:
            count_changes(t)
        if t >= 2:
            final_status(t)
        if t == RO - 1:
            at("yf")
            dma("Y", "oyf", hbm(T.yf[:]), a("ff", p=P8))
            at("yx")
            dma("Y", "oyx", hbm(T.yx[:, 0:NV]), xt(t + 1, 0, NV), 790)
        ghosts(t)
        if t < 2:
            keep_origins(t)
    at("end")
    dma("S", "oyg", hbm(T.yx[:, NV:NW]), xt(RO, NV, NW), 200)
    ops.append({"q": "Y", "fn": None, "w": [], "r": [], "grp": None, "final": True, "hold": 0.0, "late": 0.0, "tag": tuple(now)})
    _emit(g, T, _arrange(ops))
